import numpy as np, ml_dtypes
CORES = [40,64,80,88,96,104,120,144]
N = 8
BF = ml_dtypes.bfloat16
L, XS, PS, VIS, ST, SH = 128, 16, 4, 6, 1, 5
W, PN = L * XS, L * PS
def pack(x, z, c, p, q, t, w, d):
    b = lambda a: np.ascontiguousarray(a.reshape(N, 128, -1)).astype(np.float32).astype(BF)
    i = lambda a: np.ascontiguousarray(a.reshape(N, 128, -1)).astype(np.int32)
    return {"xt": b(x), "zt": b(z), "ch": i(c), "pa": i(p), "vi": i(q), "pl": i(t), "wt": i(w), "de": i(np.repeat(d.reshape(N, 8, 1), 16, axis=2))}
def parts(rng):
    top = rng.choice(np.array([3, 15, 255, 255]), (N, 8, 1, 1))
    x = rng.integers(0, top + 1, (N, 8, 16, W)); z = rng.integers(0, 256, (N, 8, 16, L))
    c, p, q = (rng.integers(0, W, (N, 8, 16, L)) for a in range(3)); q = np.where(rng.random(q.shape) < 0.1, p, q)
    t = rng.integers(0, W, (N, 8, 16, PN)); w = rng.integers(0, 256, (N, 8, 16)); d = rng.integers(3, 8, (N, 8))
    return x, z, c, p, q, t, w, d
def plant(rng, x, z, c, p, q, a, g, s):
    h = W // 2; o = rng.permutation(W); back = 37 * np.arange(16)[:, None]
    x[a, g][:, o[:h]] = rng.integers(0, 11, (16, h)); x[a, g][:, o[h:]] = rng.integers(245, 256, (16, h)); z[a, g] = 0
    e = rng.integers(0, 2, (1, L)); own, near, far = (o[rng.integers(0, h, (16, L)) + h * v] for v in (e, e, 1 - e))
    pc = np.where(s < 0, far, near); qc = np.where(s > 0, far, near)
    c[a, g] = (own - back) & (W - 1); p[a, g] = (pc - back) & (W - 1); q[a, g] = (qc - back) & (W - 1)
def small(rng, x, c, p, q, t, w, d, a, g, n):
    b = (a - ST) % N; k = np.arange(16); m = int(rng.integers(3, 7)); d[a, g] = m; w[a, g] = 0
    x[a] = x[a][:, :, :1].copy(); o = XS * int(rng.integers(0, L)) + 1; x[a, g][:, o] = 255 - x[a, g][:, o]
    hit = (o - 37 * k) & (W - 1)
    def plain(v):
        return (XS * rng.integers(0, L, (16, v)) + rng.integers(2, XS, (16, v)) - 37 * k[:, None]) & (W - 1)
    c[a, g] = plain(L); p[a, g] = plain(L); q[a, g] = plain(L); t[a, g][:, :1] = plain(1)
    lanes = 1 + rng.permutation(L - 1)[:3 * n]
    for j in range(3 * n):
        l = int(lanes[j]); r = m + (1 if j >= 2 * n else 0); st = int(rng.integers(0, 17 - r)); on = (k >= st) & (k < st + r)
        c[a, g][on, l] = hit[on]
        if j < n: q[a, g][on, l] = hit[on]
        else:
            s = np.where(on, hit, plain(1)[:, 0])
            for v in (c, p, q): v[b, g][:, l] = s
def atends(rng, hi, shape, share):
    col = rng.integers(0, 2, shape[:-2] + (1, shape[-1])); el = rng.integers(0, 2, shape)
    v = np.where(rng.random(col.shape) < 0.5, col, el) * hi
    return np.where(rng.random(shape) < share, v, rng.integers(0, hi + 1, shape))
def setup_inputs(rng):
    return pack(*parts(rng))
def setup_inputs_spread(rng):
    x, z, c, p, q, t, w, d = parts(rng)
    x = (np.exp2(8 * rng.random((N, 8, 1, W))) * rng.random((N, 8, 16, W))).astype(np.int64)
    z = (np.exp2(8 * rng.random((N, 8, 1, L))) * rng.random((N, 8, 16, L))).astype(np.int64)
    def un(shape):
        v = np.minimum(np.exp2(11 * rng.random(shape)).astype(np.int64), W) - 1
        return np.where(rng.random(shape) < 0.5, v, W - 1 - v)
    c, p, q, t = un(c.shape), un(p.shape), un(q.shape), un(t.shape)
    w = np.minimum(np.exp2(8 * rng.random(w.shape)).astype(np.int64), 256) - 1; d = np.minimum(np.exp2(4 * rng.random(d.shape)).astype(np.int64), 16)
    return pack(x, z, c, p, q, t, w, d)
def setup_inputs_ends(rng):
    x = atends(rng, 255, (N, 8, 16, W), 1.0); z = atends(rng, 255, (N, 8, 16, L), 1.0)
    one = (rng.integers(0, 16, (N, 8, 1, W)) == np.arange(16).reshape(1, 1, 16, 1)) & (rng.random((N, 8, 1, W)) < 0.3)
    x = np.where(one, np.abs(x - 1), x)
    c, p, q = (atends(rng, W - 1, (N, 8, 16, L), 0.75) for a in range(3)); t = atends(rng, W - 1, (N, 8, 16, PN), 0.85)
    w = rng.integers(0, 2, (N, 8, 16)) * 255; w[:, 1, ::2] = 0; w[:, 2] = 255; w[:, 7] = 255
    d = np.where(rng.random((N, 8)) < 0.6, 1, 16); d[:, 0] = 1; d[:, 7] = 16; d[N - 1, 2] = 16
    k = np.arange(16); hx = (37 * k) & (W - 1); hy = (((W - 1) ** 2 >> SH) + W - 1 + 37 * k) & (W - 1)
    item = np.zeros(16, np.int64); item[0] = 255; item[1] = 2
    for a in range(N):
        for g in (2, 7):
            if (a + g + N) % 2 == 0: x[a, g][:, hx] = item[:, None]; x[a, g][:, hy] = np.where(item > 0, 0, 255)[:, None]
            else: x[a, g][:, hx] = 255; x[a, g][:, hy] = 0
            for l in (2, 5, L - 1, 3, L - 2):
                down = l in (2, 5, L - 1); z[a, g][:, l] = item; c[a, g][:, l] = 0
                p[a, g][:, l] = W - 1 if down else 0; q[a, g][:, l] = 0 if down else W - 1
    return pack(x, z, c, p, q, t, w, d)
def setup_inputs_corners(rng):
    x, z, c, p, q, t, w, d = parts(rng); k = np.arange(16)[:, None]
    tie = np.array([0, 0, -1, -1, 0, 0, 1, 1, 0, -1, -1, 0, 1, 1, 0, 1])
    for a in range(N):
        for g in range(8):
            case = (g + a) % 8
            if a == 1: case = (0, 2)[g % 2]
            if a == 2: case = (1, 3, 4)[g % 3]
            if a > 2 and a % 2 == 1 and case == 7: case = 0
            n = int(rng.integers(2, 8)); st = rng.integers(0, 17 - n, (1, L)); s = np.full((16, L), -1); d[a, g] = 16
            if case < 2: s = np.where((k >= st) & (k < st + n), -1, 1); d[a, g] = n + case
            if case == 3: s = np.full((16, L), 1); d[a, g] = 1
            if case == 4: s = np.zeros((16, L), np.int64); d[a, g] = 1
            if case == 5: s = tie[(k + rng.integers(0, 16, (1, L))) % 16]; d[a, g] = 2
            if case == 6: s = np.where(k == 15 * rng.integers(0, 2, (1, L)), -1, 1); d[a, g] = 1
            if case == 7: s[:, int(rng.integers(0, L))] = 0
            plant(rng, x, z, c, p, q, a, g, s)
            j = int(rng.integers(0, 4))
            if j == 0: w[a, g] = 0
            if j == 1: w[a, g] = 255
            if j == 2: w[a, g] = 0; w[a, g, int(rng.integers(0, 16))] = 1
    return pack(x, z, c, p, q, t, w, d)
def setup_inputs_crowd(rng):
    x, z, c, p, q, t, w, d = parts(rng); few = np.array([0, W - 1, W // 2, 3])
    for a in range(N):
        for g in range(8):
            if a in (0, 2):
                plant(rng, x, z, c, p, q, a, g, np.full((16, L), -1)); d[a, g] = int(rng.integers(3, 7))
                for v in (c, p, q): v[a, g] = v[a, g][:, :1].copy()
                if a == 2 and g == 7: l = int(rng.integers(0, L)); p[a, g][:, l] = c[a, g][:, l]; q[a, g][:, l] = c[a, g][:, l]
            elif g % 2 == 0:
                for v in (c, p, q): v[a, g] = rng.choice(few, (16, L))
                z[a, g] = z[a, g][:, rng.integers(0, 4, L)]
            else:
                t[a, g] = t[a, g][:, rng.integers(0, 3, PN)]
                if g == 3: x[a, g] = x[a, g][:, :1].copy()
                if g == 5: y = x[a, g][:, 1].copy(); x[a, g] = x[a, g][:, :1].copy(); x[a, g][:, int(rng.integers(0, W))] = y
    return pack(x, z, c, p, q, t, w, d)
def setup_inputs_close(rng):
    x, z, c, p, q, t, w, d = parts(rng); m = rng.integers(0, 256, (N, 8, 16, 1))
    x = np.where(rng.random((N, 8, 1, W)) < 0.5, m, 255 - m)
    e = (rng.integers(0, 16, (N, 8, 1, W)) == np.arange(16).reshape(1, 1, 16, 1)) * rng.integers(-1, 2, (N, 8, 1, W))
    x = np.clip(x + e, 0, 255); d = rng.integers(1, 6, (N, 8)); gs = rng.permutation(8)
    small(rng, x, c, p, q, t, w, d, 1, int(gs[0]), 1)
    small(rng, x, c, p, q, t, w, d, 3, int(gs[1]), 3)
    return pack(x, z, c, p, q, t, w, d)
def check_inputs(d):
    bad = []
    for k, lo, hi in (("xt", 0, 255), ("zt", 0, 255), ("ch", 0, W - 1), ("pa", 0, W - 1), ("vi", 0, W - 1), ("pl", 0, W - 1), ("wt", 0, 255), ("de", 1, 16)):
        v = np.asarray(d[k]).astype(np.float64)
        if not (np.min(v) >= lo and np.max(v) <= hi): bad.append("range of " + k)
        elif np.any(v != np.floor(v)): bad.append("whole numbers in " + k)
    v = np.asarray(d["de"]).reshape(N, 8, 16)
    if np.any(v != v[:, :, :1]): bad.append("de alike in a group")
    return bad
def reference(xt, zt, ch, pa, vi, pl, wt, de):
    x = xt.astype(np.float32).astype(np.int32).reshape(N, 8, 16, W); z = zt.astype(np.float32).astype(np.int64).reshape(N, 8, 16, L)
    c, p, q = (a.astype(np.int64).reshape(N, 8, 16, L) for a in (ch, pa, vi)); t = pl.astype(np.int64).reshape(N, 8, 16, PN)
    w = wt.astype(np.int64).reshape(N, 8, 16, 1); d = de.astype(np.int64).reshape(N, 8, 16)[:, :, :1]
    site = np.arange(16).reshape(1, 1, 16, 1); k = np.arange(16); lane = np.arange(L); count = np.zeros((N, 1, 1), np.int64)
    for visit in range(VIS):
        if visit > 0: q = np.roll(q, ST, axis=0)
        u = np.add.reduce(w * z, axis=2) & (W - 1)
        got = []
        for n in (c, p, q):
            h = (((n * u[:, :, None]) >> SH) + n + 37 * site) & (W - 1)
            ix = np.ascontiguousarray(h.transpose(0, 1, 3, 2)).reshape(N, 8, 1, 16 * L)
            got.append(np.take_along_axis(x, ix, 3).reshape(N, 8, 16, L, 16))
        xs, ys, vs = got
        s = np.sign(np.add.reduce(np.abs(xs - vs), axis=2) - np.add.reduce(np.abs(xs - ys), axis=2)).astype(np.int64)
        H = np.zeros((N, 8, L), np.int64); top = H; ti = H; best = H - 99; bi = H; bj = H
        for j in range(1, 17):
            H = H + s[..., j - 1]; e = top - H; win = e > best
            best = np.where(win, e, best); bi = np.where(win, ti, bi); bj = np.where(win, j, bj)
            ge = H >= top; top = np.where(ge, H, top); ti = np.where(ge, j, ti)
        run = (k >= bi[..., None]) & (k < bj[..., None])
        m = np.max(np.where(run[:, :, None], xs, 0), axis=4).astype(np.int64)
        um = np.add.reduce(w * m, axis=2) & (W - 1)
        rec = best >= d + (count & 1)
        cut = run.transpose(0, 1, 3, 2) & rec[:, :, None]
        c, q = np.where(cut, p, c), np.where(cut, c, q)
        p = np.take_along_axis(t, (um & (PN - 1))[:, :, None], 3)
        at = (PS * lane + (um & (PS - 1)))[:, :, None]
        np.put_along_axis(t, at, np.where(rec[:, :, None], c, np.take_along_axis(t, at, 3)), 3)
        ib = bi[:, :, None, :, None]
        xi = np.take_along_axis(xs, ib, 4)[..., 0]; vv = np.take_along_axis(vs, ib, 4)[..., 0]
        np.put_along_axis(x, (XS * lane + (um & (XS - 1)))[:, :, None], (xi + vv) >> 1, 3)
        z = (z + m) >> 1
        count = np.add.reduce(rec.reshape(N, 8 * L).astype(np.int64), axis=1).reshape(N, 1, 1)
    return {"yc": c.reshape(N, 128, L).astype(np.float32), "yp": p.reshape(N, 128, L).astype(np.float32), "yq": q.reshape(N, 128, L).astype(np.float32),
            "yl": t.reshape(N, 128, PN).astype(np.float32), "yx": x.reshape(N, 128, W).astype(np.float32).astype(BF), "yz": z.reshape(N, 128, L).astype(np.float32).astype(BF)}

@@ -1,0 +1,538 @@
+from concourse.bass import DstId, RemoteDMATransfer
+from concourse.mybir import dt, AluOpType, AxisListType, ActivationFunctionType
+
+A = AluOpType
+F = ActivationFunctionType
+VIS = 6
+TAIL = [("x", 0), ("t", 0), ("x", 1), ("t", 1), ("t", 2), ("t", 3), ("t", 4), ("t", 5), ("t", 7), ("x", 2), ("t", 6)]
+PLAN = [("X", "x", 0, 4), ("X", "x", 4, 8), ("X", "x", 8, 12), ("X", "x", 12, 16), ("preC",),
+        ("i", "y", 0), ("f", 0), ("i", "y", 1), ("f", 1), ("i", "y", 2), ("f", 2),
+        ("d", "y", 0, 4), ("d", "y", 4, 8), ("d", "y", 8, 12), ("d", "y", 12, 16),
+        ("b", "y", 0, 4), ("b", "y", 4, 8), ("i", "v", 0), ("preQ",), ("b", "y", 8, 12),
+        ("f", 3), ("i", "v", 1), ("i", "v", 2), ("b", "y", 12, 16),
+        ("g", "v", 13, 16, "B1"), ("d", "v", 0, 3), ("b", "v", 0, 3), ("d", "v", 3, 7), ("c", "v", 13, 16, "B1"),
+        ("b", "v", 3, 7), ("d", "v", 7, 10), ("d", "v", 10, 12), ("b", "v", 7, 10), ("d", "v", 12, 13),
+        ("l", "v", 12, 13), ("b", "v", 10, 12), ("r", "v", 12, 13), ("f", 4)]
+MAG = 12582912.0
+MAG11 = 1.5 * 2.0 ** 34
+
+SCRATCH = {}
+
+
+def _decl(names, cols, dtype, where="sbuf"):
+    for n in names.split():
+        SCRATCH[n] = (where, [128, cols], dtype)
+
+
+_decl("X DV DY AV AY SC MK CUT", 2048, "bfloat16")
+_decl("TAB", 2048 + 768, "bfloat16")
+_decl("VAL", 176, "bfloat16")
+_decl("OT", 12, "uint16")
+_decl("POOL", 1024, "float32")
+_decl("PLI", 512, "int32")
+_decl("S30 S31 S32 S33 S34 S35 S36", 384, "float32")
+_decl("EAR EL", 256, "float32")
+_decl("CI PI_ QI Hx Hy Hv Gx Gy Gv", 128, "int32")
+_decl("ZB ZR ONESB IB NIB I2B I4K IN2K GX GD CT MM YZ", 128, "bfloat16")
+_decl("Z2 WM J16 C1 C2A C2B I16", 128, "float16")
+_decl("G KP GEP D0 C128 I32 NI32 ZZ FU SG S1 S2 RQ RC QO FS TQ", 128, "float32")
+_decl("GE", 144, "float32")
+_decl("EBP EBN EB2P EB2N WE", 144, "bfloat16")
+_decl("IX IY IV", 128, "uint16")
+_decl("PERM OI OE OC OC0 CL OR OP", 8, "uint16")
+_decl("K A1 A2 S CD KI A15 A511 A3", 8, "int32")
+_decl("B8 BT BP BOFF AT NB AP CJ", 8, "float32")
+_decl("NN", 8, "bfloat16")
+_decl("LE", 16, "float32")
+_decl("WI DI", 4, "int32")
+_decl("PN KN R7 R8", 1, "int32")
+_decl("CF", 24, "float32")
+_decl("B0 B1 B2 B3 B4 B5 B6 B7", 512, "float32", "psum")
+
+EXT = 560
+LOADS = ["wt", "zt", "ch", "pa", "de", "vi", "pl", "xt", "x2"]
+STORES = ["yc", "yp", "yq", "yl", "yx", "yz"]
+SEMAPHORES = (["sv", "sa", "sp", "sg", "ls"] + ["l_" + n for n in LOADS] + ["o_" + n for n in STORES]
+              + ["m%d" % i for i in range(VIS)])
+
+PF, KF, G16, T7, PB, C37, CA, CE, C16, WF, WH, CTHR, THR, CNT, CB1, CF1, CF2 = range(17)
+
+
+def message(T, i):
+    if i == 0:
+        return ("EAR", 0, 256), ("EL", 0, 256)
+    if i == 1:
+        return ("OC0", 0, 8), ("CL", 0, 8)
+    return ("QO", 0, 128), ("S3%d" % i, 256, 384)
+
+
+def route(T, topo, r):
+    src = T.cores[r]
+    dst = T.cores[(r + 1) % len(T.cores)]
+    if topo.may_write(src, dst):
+        return [src, dst]
+    cand = [c for c in topo.cores_of(src) if c != src and T.rank_of(c) is None and topo.may_write(c, dst)]
+    near = [c for c in cand if topo.die(c) == topo.die(src)]
+    return [src, (near or cand)[0], dst]
+
+
+def relay_program(g, core, T, topo, src, dst):
+    n_in = len(topo.engines(src, core))
+    n_out = len(topo.engines(core, dst))
+    rid, pid = topo.addr(dst, core)
+    for i in range(VIS):
+        n, a, b = message(T, i)[1]
+        g.wait_ge(T.sem["m%d" % i], n_in)
+        g.remote_dma(T[n][:, a:b], T[n][:, a:b], T.sem["m%d" % i], T.sem.ls, pid, rid, topo.mask(core, dst))
+    g.wait_ge(T.sem.ls, n_out * VIS)
+
+
+def rank_program(g, core, T, topo):
+    rank = T.rank_of(core)
+    nr = len(T.cores)
+    if rank is None:
+        for r in range(nr):
+            way = route(T, topo, r)
+            if len(way) == 3 and way[1] == core:
+                relay_program(g, core, T, topo, way[0], way[2])
+        return
+    nxt = route(T, topo, rank)[1]
+    prv = route(T, topo, (rank - 1) % nr)[-2]
+    n_out = len(topo.engines(core, nxt))
+    n_in = len(topo.engines(prv, core))
+    rid, pid = topo.addr(nxt, core)
+
+    Q = {"v": g.vector, "a": g.scalar, "p": g.tensor, "g": g, "s": g.sync}
+    cnt = {}
+    seen = {e: {} for e in Q}
+    acc = {}
+
+    def touch(e, regs, wr, need):
+        for (n, lo, hi) in regs:
+            ps = SCRATCH[n][0] == "psum"
+            for (l2, h2, w2, e2, s2, c2) in acc.get(n, []):
+                if ps:
+                    hit = (e2 != e) or (e != "p" and (wr or w2))
+                else:
+                    hit = l2 < hi and lo < h2 and (wr or w2)
+                if hit and need.get(s2, 0) < c2:
+                    need[s2] = c2
+
+    def note(e, regs, wr, s, c):
+        for (n, lo, hi) in regs:
+            old = acc.get(n, [])
+            if wr:
+                old = [x for x in old if not (lo <= x[0] and x[1] <= hi)]
+            else:
+                old = [x for x in old if not (x[3] == e and x[4] == s and not x[2] and lo <= x[0] and x[1] <= hi)]
+            old.append((lo, hi, wr, e, s, c))
+            acc[n] = old
+
+    def op(e, fn, rd, wr, sem=None, inc=1, attach=True):
+        need = {}
+        touch(e, rd, False, need)
+        touch(e, wr, True, need)
+        for s2 in sorted(need):
+            if seen[e].get(s2, 0) < need[s2]:
+                Q[e].wait_ge(T.sem[s2], need[s2])
+                seen[e][s2] = need[s2]
+        s = sem or ("s" + e)
+        ins = fn()
+        if attach:
+            ins.then_inc(T.sem[s], inc)
+        cnt[s] = cnt.get(s, 0) + inc
+        note(e, rd, False, s, cnt[s])
+        note(e, wr, True, s, cnt[s])
+
+    def ap(r):
+        if len(r) == 4:
+            return T[r[0]][:, r[1]:r[2]:r[3]]
+        return T[r[0]][:, r[1]:r[2]]
+
+    def R(n, lo=0, hi=None, st=None):
+        if hi is None:
+            hi = SCRATCH[n][1][1]
+        return (n, lo, hi) if st is None else (n, lo, hi, st)
+
+    def col(c):
+        return ("CF", c, c + 1)
+
+    def r3(x):
+        return x[:3]
+
+    def src(x):
+        if isinstance(x[0], tuple):
+            return ap(x[0]).indirect(ap(x[1])), [r3(x[0]), r3(x[1])]
+        return ap(x), [r3(x)]
+
+    def dstp(x):
+        if isinstance(x[0], tuple):
+            return ap(x[0]).indirect(ap(x[1])), [r3(x[0])], [r3(x[1])]
+        return ap(x), [r3(x)], []
+
+    def scal(s):
+        if isinstance(s, tuple):
+            return ap(s), [r3(s)]
+        return s, []
+
+    def cp(out, in_):
+        o, w, r0 = dstp(out)
+        i, r1 = src(in_)
+        op("v", lambda: g.vector.tensor_copy(o, i), r0 + r1, w)
+
+    def tt(out, in0, in1, alu):
+        i, r1 = src(in0)
+        op("v", lambda: g.vector.tensor_tensor(ap(out), i, ap(in1), alu), r1 + [r3(in1)], [r3(out)])
+
+    def ts(out, in0, s1, o0, s2=None, o1=None):
+        a1, r1 = scal(s1)
+        a2, r2 = scal(s2)
+        i, r0 = src(in0)
+        if o1 is None:
+            fn = lambda: g.vector.tensor_scalar(ap(out), i, a1, None, o0)
+        else:
+            fn = lambda: g.vector.tensor_scalar(ap(out), i, a1, a2, o0, o1)
+        op("v", fn, r0 + r1 + r2, [r3(out)])
+
+    def scan(out, d0, d1, init, o0, o1):
+        op("v", lambda: g.vector.tensor_tensor_scan(ap(out), ap(d0), ap(d1), init, o0, o1), [r3(d0), r3(d1)], [r3(out)])
+
+    def mset(out, v):
+        op("v", lambda: g.vector.memset(ap(out), v), [], [r3(out)])
+
+    def act(out, in_, func=F.Identity, bias=0.0, scale=1.0, accum=None):
+        i, r1 = src(in_)
+        b, r2 = scal(bias)
+        s, r4 = scal(scale)
+        if accum is None:
+            op("a", lambda: g.scalar.activation(ap(out), i, func, bias=b, scale=s), r1 + r2 + r4, [r3(out)])
+        else:
+            op("a", lambda: g.scalar.activation(ap(out), i, func, bias=b, scale=s, accum_out=ap(accum)),
+               r1 + r2 + r4, [r3(out), r3(accum)])
+
+    def mm(out, lhs, rhs, start, stop):
+        op("p", lambda: g.tensor.matmul(ap(out), ap(lhs), ap(rhs), start, stop), [r3(lhs), r3(rhs)], [r3(out)])
+
+    def iota(out, pat, base, cm, flag=True):
+        if flag:
+            fn = lambda: g.iota(ap(out), pat, base, cm, allow_small_or_imprecise_dtypes=True)
+        else:
+            fn = lambda: g.iota(ap(out), pat, base, cm)
+        op("g", fn, [], [r3(out)])
+
+    def load(e, name, out):
+        op(e, lambda: Q[e].dma_start(ap(out), T[name][:]), [], [out], "l_" + name, 16)
+
+    def store(e, name, in_):
+        op(e, lambda: Q[e].dma_start(T[name][:], ap(in_)), [in_], [], "o_" + name, 16)
+
+    def send(i):
+        s, d = message(T, i)
+        op("g", lambda: g.remote_dma(ap(d), ap(s), T.sem["m%d" % i], T.sem.ls, pid, rid, topo.mask(core, nxt)),
+           [s], [], "ls", n_out, False)
+
+    for i in range(VIS):
+        cnt["m%d" % i] = n_in
+        note("r", [message(T, i)[1]], True, "m%d" % i, n_in)
+
+    def P_(t):
+        return R("S3%d" % t, 0, 128)
+
+    def C_(t):
+        return R("S3%d" % t, 128, 256)
+
+    def V_(t):
+        return R("S3%d" % t, 256, 384)
+
+    U1, U2 = R("B1", 0, 128), R("B2", 0, 128)
+
+    load("s", "wt", R("WI", 0, 1))
+    load("s", "zt", R("ZB"))
+    load("s", "ch", R("CI"))
+    load("a", "xt", R("TAB", 0, 2048))
+    ext = R("TAB", 2048, 2048 + EXT)
+    op("a", lambda: g.scalar.dma_start(ap(ext), T.xt[:, 0:EXT]), [], [ext], "l_x2", 16)
+    load("s", "pa", R("PI_"))
+    load("s", "vi", R("QI"))
+    load("s", "de", R("DI", 0, 1))
+    load("s", "pl", R("PLI"))
+    iota(R("PN"), [[0, 1]], 0, 1, False)
+    iota(R("G"), [[16, 8], [0, 16]], 0, 0)
+    iota(R("B8"), [[1, 8]], 0, 0)
+    iota(R("GE"), [[1, 144]], -16, 0)
+    iota(R("KP"), [[0, 8], [1, 16]], 0, 0)
+    iota(R("MK"), [[0, 2048]], 1, 0)
+    mset(R("CUT"), 0.0)
+    ts(R("KN"), R("PN"), 15, A.bitwise_and)
+    cp(col(PF), R("PN"))
+    cp(col(KF), R("KN"))
+    ts(R("R7"), R("PN"), 7, A.bitwise_and)
+    tt(col(G16), col(PF), col(KF), A.subtract)
+    ts(R("GEP", 0, 16), R("KP", 0, 16), col(KF), A.is_le)
+    ts(R("LE"), R("KP", 0, 16), col(KF), A.add, 15.0, A.is_le)
+    ts(R("C2A"), R("G"), 0.0, A.mult, -1023.5 / 16, A.add)
+    ts(R("C2B"), R("G"), 0.0, A.mult, 2.0, A.add)
+    ts(R("J16"), R("G"), col(G16), A.is_equal)
+    ts(R("I32"), R("GE", 16, 144), col(PF), A.is_equal)
+    ts(R("R8"), R("PN"), 3, A.logical_shift_right, 1, A.bitwise_and)
+    ts(col(T7), R("R7"), 16.0, A.mult)
+    ts(R("EBP"), R("GE"), col(G16), A.is_equal, 16384.0, A.mult)
+    ts(col(WH), R("WI", 0, 1), 0.5, A.mult)
+    ts(R("Z2"), R("ZB"), 2.0, A.mult)
+    ts(R("WM"), R("G"), col(G16), A.is_equal, col(WH), A.mult)
+    tt(col(PB), col(T7), R("R8"), A.add)
+    cp(C_(0), R("CI"))
+    ts(col(C37), col(KF), 37.0, A.mult)
+    ts(R("PERM"), R("B8"), 2.0, A.mult, col(PB), A.add)
+
+    act(col(CA), col(KF), scale=128.0)
+    act(col(CE), col(KF), scale=128.0, bias=127.0)
+    act(col(C16), col(KF), scale=16.0)
+    act(R("BOFF"), R("B8"), scale=524288.0)
+    act(R("D0"), R("G"), scale=32641.0, bias=30720.0)
+    act(R("BT"), R("B8"), scale=256.0, bias=col(C16))
+    act(R("BP"), R("BT"), scale=0.25)
+    for e1 in range(16):
+        act(R("CUT", 128 * e1, 128 * e1 + 16), R("GEP", 0, 16), F.Copy, scale=R("LE", e1, e1 + 1))
+    act(R("NI32"), R("I32"), scale=-1.0)
+    act(R("EBN"), R("EBP"), scale=-1.0)
+    for tk in PLAN:
+        if tk[:2] == ("r", "v"):
+            act(R("EB2P"), R("EBP"), scale=2.0)
+            break
+    for tk in PLAN:
+        if tk[:2] == ("r", "y"):
+            act(R("EB2N"), R("EBP"), scale=-2.0)
+            break
+    act(R("IB"), R("I32"))
+    act(R("NIB"), R("I32"), scale=-1.0)
+    act(R("I2B"), R("I32"), scale=2.0)
+    act(R("I4K"), R("I32"), scale=4096.0)
+    act(R("IN2K"), R("I32"), scale=-2048.0)
+    act(R("ZZ"), R("ZB"), bias=2047.5)
+
+    def u_pre():
+        mm(U1, R("J16"), R("C2A"), True, False)
+        mm(U1, R("WM"), R("C1"), False, False)
+        mm(U2, R("J16"), R("C2B"), True, False)
+        mm(U2, R("WM"), R("C1"), False, False)
+
+    def u_main():
+        mm(U1, R("WM"), R("Z2"), False, True)
+        mm(U2, R("WM"), R("Z2"), False, True)
+
+    def idx_steps(n, s):
+        return [lambda: tt(R("H" + s), U2, n, A.mult),
+                lambda: ts(R("G" + s), R("H" + s), 5, A.logical_shift_right, 2047, A.bitwise_and),
+                lambda: ts(R("I" + s.upper()), (R("G" + s), R("PERM")), col(C37), A.add)]
+
+    def u_mod():
+        ts(R("FU"), U1, MAG11, A.add, MAG11, A.subtract)
+        tt(U2, U2, R("FU"), A.subtract)
+
+    def weave(*chains):
+        k = max(len(c) for c in chains)
+        for i in range(k):
+            for c in chains:
+                if i < len(c):
+                    c[i]()
+
+    mm(U1, R("J16"), R("C2A"), True, False)
+    mm(U2, R("J16"), R("C2B"), True, False)
+    u_main()
+    ts(R("FU"), U1, MAG11, A.add, MAG11, A.subtract)
+    cp(col(WF), R("WI", 0, 1))
+    tt(U2, U2, R("FU"), A.subtract)
+    mset(R("ZR"), 0.0)
+    weave(idx_steps(C_(0), "x"),
+          [lambda: cp(P_(0), R("PI_")),
+           lambda: cp(R("EAR", 128, 256), R("QI")),
+           lambda: mset(R("ONESB"), 1.0)])
+    late = [lambda: ts(R("I16"), R("GE", 16, 144), col(PF), A.is_equal),
+            lambda: ts(R("WE"), R("GE"), col(G16), A.is_equal, col(WF), A.mult),
+            lambda: ts(R("C1"), R("G"), 0.0, A.mult, -2048.0, A.add),
+            lambda: mset(R("C128"), 128.0)]
+
+    def dmm(a, buf, eb, start, stop):
+        mm(R("B0", 0, 128), R(eb, 16 - a, 144 - a), R(buf, 128 * a, 128 * a + 128), start, stop)
+
+    n_dmm = sum(tk[3] - tk[2] for tk in PLAN if tk[0] in ("l", "r", "b", "c"))
+    plain_v = [a for tk in PLAN if tk[0] == "g" and tk[1] == "v" for a in range(tk[2], tk[3])]
+
+    for t in range(VIS):
+        last = t == VIS - 1
+        qsel = t > 0
+        vq = V_(t) if t > 0 else R("EAR", 128, 256)
+        ix = {"y": idx_steps(P_(t), "y"), "v": idx_steps(vq, "v")}
+        if t == 0:
+            fill = [lambda: tt(R("EAR", 0, 128), C_(0), R("EAR", 128, 256), A.subtract),
+                    lambda: send(0),
+                    lambda: ts(col(CTHR), R("DI", 0, 1), 16384.0, A.mult, 16384.0, A.add),
+                    lambda: tt(R("D0"), R("D0"), R("KP"), A.add),
+                    lambda: cp(R("POOL", 0, 512), R("PLI"))]
+        else:
+            fill = [lambda: ts(R("A3"), R("KI"), 3, A.bitwise_and),
+                    lambda: tt(R("NB"), R("NN"), R("BP"), A.add),
+                    lambda: tt(R("AP"), R("A3"), R("NB"), A.add),
+                    lambda: cp(R("OP"), R("AP")),
+                    lambda: cp((R("POOL"), R("OP")), C_(t))]
+        done = [0]
+
+        def dsum(a, buf, eb):
+            dmm(a, buf, eb, done[0] == 0, done[0] == n_dmm - 1)
+            done[0] += 1
+
+        for tk in PLAN:
+            kind = tk[0]
+            if kind == "f":
+                fill[tk[1]]()
+            elif kind == "i":
+                if t == 1 and tk[1:] == ("v", 0):
+                    tt(R("TQ"), (R("CUT"), R("CL")), R("EL", 0, 128), A.mult)
+                    tt(vq, R("TQ"), R("EL", 128, 256), A.add)
+                ix[tk[1]][tk[2]]()
+                if t == 0 and tk[1] == "v":
+                    late[tk[2]]()
+                    if tk[2] == 2:
+                        late[3]()
+            elif kind == "preC":
+                mm(R("B5", 0, 128), R("I32"), P_(t), True, False)
+                mm(R("B5", 0, 128), R("NI32"), C_(t), False, False)
+                mm(R("B6", 0, 128), R("I32"), C_(t), True, False)
+                if qsel:
+                    mm(R("B3", 0, 128), R("I32"), C_(t), True, False)
+            elif kind == "preQ":
+                if qsel:
+                    mm(R("B3", 0, 128), R("NI32"), vq, False, False)
+                    mm(R("B4", 0, 128), R("I32"), vq, True, False)
+            else:
+                s_, a0, a1 = tk[1], tk[2], tk[3]
+                lo, hi = 128 * a0, 128 * a1
+                dd, aa = ("DY", "AY") if s_ == "y" else ("DV", "AV")
+                lst = (R("TAB", 0, 2048 + EXT), R("I" + s_.upper(), 8 * a0, 8 * a1))
+                one, two, lin = ("EBN", "EB2N", "EBP") if s_ == "y" else ("EBP", "EB2P", "EBN")
+                if kind == "X":
+                    act(R("X", lo, hi), lst, F.Copy)
+                elif kind == "d":
+                    tt(R(dd, lo, hi), lst, R("X", lo, hi), A.subtract)
+                elif kind == "l":
+                    for a in range(a0, a1):
+                        dsum(a, dd, lin)
+                elif kind == "r":
+                    ts(R(aa, lo, hi), R(dd, lo, hi), 0.0, A.max)
+                    for a in range(a0, a1):
+                        dsum(a, aa, two)
+                elif kind == "b":
+                    act(R(aa, lo, hi), R(dd, lo, hi), F.Abs)
+                    for a in range(a0, a1):
+                        dsum(a, aa, one)
+                elif kind == "g":
+                    act(R(dd, lo, hi), lst, F.Copy)
+                    mm(R(tk[4], 0, hi - lo), R("NIB"), R("X", lo, hi), True, False)
+                    mm(R(tk[4], 0, hi - lo), R("IB"), R(dd, lo, hi), False, True)
+                elif kind == "c":
+                    act(R(aa, lo, hi), R(tk[4], 0, hi - lo), F.Abs)
+                    for a in range(a0, a1):
+                        dsum(a, aa, one)
+        if not last:
+            u_pre()
+        oc = R("OC0") if t == 0 else R("OC")
+        thr = col(CTHR) if t == 0 else col(THR)
+        ts(R("SG"), R("B0", 0, 128), -16384.0, A.max, 16384.0, A.min)
+        scan(R("S1"), R("D0"), R("SG"), 0.0, A.max, A.subtract)
+        scan(R("S2"), R("C128"), R("S1"), 0.0, A.add, A.max)
+        tt(R("K"), R("S2", 15, 128, 16), R("BOFF"), A.subtract)
+        ts(R("A1"), R("K"), 127, A.bitwise_and)
+        ts(R("S"), R("K"), thr, A.subtract, -1.0, A.max)
+        ts(R("OI"), R("A1"), col(CA), A.add)
+        ts(R("CD"), R("S"), 0x78F, A.bitwise_and)
+        ts(R("A2"), R("K"), 7, A.logical_shift_right, 127, A.bitwise_and)
+        cp(oc, R("CD"))
+        cp((R("MK"), R("OI")), R("ZR"))
+        ts(R("OE"), R("A2"), -1.0, A.mult, col(CE), A.add)
+        scan(R("SC"), R("MK"), R("X"), 0.0, A.mult, A.max)
+        if t == 0:
+            send(1)
+        act(R("CT"), (R("CUT"), oc), F.Copy)
+        if qsel:
+            mm(R("B3", 0, 128), R("I4K"), R("CT"), False, True)
+        mm(R("B5", 0, 128), R("I4K"), R("CT"), False, True)
+        if qsel:
+            mm(R("B4", 0, 128), R("IN2K"), R("CT"), False, False)
+        mm(R("B6", 0, 128), R("IN2K"), R("CT"), False, False)
+        act(R("GX"), (R("X"), R("OI")), F.Copy)
+        if qsel:
+            act(R("RQ"), R("B3", 0, 128), F.Relu, bias=-2048.0)
+            mm(R("B4", 0, 128), R("I32"), R("RQ"), False, True)
+        act(R("RC"), R("B5", 0, 128), F.Relu, bias=-2048.0)
+        mm(R("B6", 0, 128), R("I32"), R("RC"), False, True)
+        act(R("GD"), (R("DV"), R("OI")), F.Copy)
+        mm(R("B7", 0, 128), R("I2B"), R("GX"), True, False)
+        for a in plain_v:
+            mm(R("B7", a, 128, 16), R("NIB"), R("GX", a, 128, 16), False, False)
+        mm(R("B7", 0, 128), R("IB"), R("GD"), False, True)
+        if qsel:
+            act(R("QO"), R("B4", 0, 128), F.Copy)
+            if last:
+                store("s", "yq", R("QO"))
+            else:
+                send(t + 1)
+        act(C_(t + 1), R("B6", 0, 128), F.Copy)
+        if last:
+            store("s", "yc", C_(t + 1))
+        else:
+            iota(R("MK"), [[0, 2048]], 1, 0)
+        act(R("MM"), (R("SC"), R("OE")), F.Copy)
+        tt(R("Z2"), (R("SC"), R("OE")), R("ZZ"), A.add)
+        ts(R("NN"), R("S"), 0.0, A.is_lt, 512.0, A.mult)
+        act(R("FS"), R("B7", 0, 128), scale=0.4995, bias=MAG)
+        act(R("VAL", 0, 128), R("FS"), bias=-MAG)
+        if not last:
+            act(R("VAL", 128, 176), R("FS", 0, 48), bias=-MAG)
+            u_main()
+        for a in range(16):
+            mm(R("B0", 0, 8), R("WE", 16 - a, 144 - a), R("MM", a, 128, 16), a == 0, a == 15)
+        mm(R("B7", 0, 128), R("I16"), R("Z2"), True, True)
+        tab = [lambda: cp(R("KI"), R("B0", 0, 8)),
+               lambda: ts(R("A15"), R("KI"), 15, A.bitwise_and),
+               lambda: ts(R("A511"), R("KI"), 511, A.bitwise_and),
+               lambda: tt(R("AT"), R("A15"), R("BT"), A.add),
+               lambda: cp(R("OR"), R("A511")),
+               lambda: cp(R("OT", 0, 8), R("AT")),
+               lambda: cp((R("TAB"), R("OT", 0, 8 if last else 11)), R("VAL", 0, 128 if last else 176)),
+               lambda: ts(R("OT", 8, 11), R("AT", 0, 3), 2048.0, A.add)]
+        if not last:
+            u_mod()
+            x4 = idx_steps(C_(t + 1), "x")
+            for (w_, i_) in TAIL:
+                (x4 if w_ == "x" else tab)[i_]()
+            act(R("ZZ"), R("B7", 0, 128), scale=0.5, bias=1023.5)
+            mm(R("B7", 0, 8), R("ONESB"), R("NN"), True, True)
+            act(P_(t + 1), (R("POOL", 0, 512), R("OR")), F.Copy)
+            act(R("CJ"), R("B7", 0, 8), scale=1.0 / 512, accum=col(CNT))
+            act(col(CF1), col(CNT), scale=0.4999, bias=MAG)
+            act(col(CB1), col(CNT), scale=16384.0, bias=col(CTHR))
+            act(col(CF2), col(CF1), bias=-MAG)
+            act(col(THR), col(CF2), scale=-32768.0, bias=col(CB1))
+        else:
+            tt(R("NB"), R("NN"), R("BP"), A.add)
+            tab[0]()
+            tab[1]()
+            tab[2]()
+            tab[3]()
+            tab[4]()
+            tab[5]()
+            ts(R("A3"), R("KI"), 3, A.bitwise_and)
+            tab[6]()
+            store("s", "yx", R("TAB", 0, 2048))
+            tt(R("AP"), R("A3"), R("NB"), A.add)
+            cp(R("OP"), R("AP"))
+            act(R("YZ"), R("B7", 0, 128), scale=0.5, bias=-1024.0)
+            act(P_(t + 1), (R("POOL", 0, 512), R("OR")), F.Copy)
+            cp((R("POOL"), R("OP")), C_(t + 1))
+            store("a", "yz", R("YZ"))
+            store("a", "yp", P_(t + 1))
+            store("a", "yl", R("POOL", 0, 512))
+
+    for s in sorted(cnt):
+        g.wait_ge(T.sem[s], cnt[s])

@@ -4,15 +4,21 @@ from concourse.mybir import dt, AluOpType, AxisListType, ActivationFunctionType
 A = AluOpType
 F = ActivationFunctionType
 VIS = 6
-TAIL = [("x", 0), ("t", 0), ("x", 1), ("t", 1), ("t", 2), ("t", 3), ("t", 4), ("t", 5), ("t", 7), ("x", 2), ("t", 6)]
+MAG4 = 1.5 * 2.0 ** 27
+CUTS = ("S1a S2a SGb mM0 Ka S1b A1a A2a S2b OIa OEa Kb MKa S A1b A2b CD OIb OEb OC MKb SCa SCb Z2a "
+        "GXa GDa CT mQ1 mQ2 mC1 mC2 GXb RQ MMa")
+TAIL = ("mQ3 RC MMb Z2b mU mM QO IO PS mC3 GDb mS CN FS VAL VAL2 "
+        "FU SU NN UU mN F16 T2 KI x0 AT A511 x1 OT OT2 OR x2 TAB mZ CJ c1 c2 c3 PN c4 ZZ")
+LAST = ("RC GDb mS MMb PS NN Z2b NB mM mQ3 mC3 FS VAL CN QO mZ "
+        "SU F16 T2 KI AT A511 A3 OT OR ZZ AP TAB OP PN PL")
 PLAN = [("X", "x", 0, 4), ("X", "x", 4, 8), ("X", "x", 8, 12), ("X", "x", 12, 16), ("preC",),
         ("i", "y", 0), ("f", 0), ("i", "y", 1), ("f", 1), ("i", "y", 2), ("f", 2),
-        ("d", "y", 0, 4), ("d", "y", 4, 8), ("d", "y", 8, 12), ("d", "y", 12, 16),
-        ("b", "y", 0, 4), ("b", "y", 4, 8), ("i", "v", 0), ("preQ",), ("b", "y", 8, 12),
-        ("f", 3), ("i", "v", 1), ("i", "v", 2), ("b", "y", 12, 16),
-        ("g", "v", 13, 16, "B1"), ("d", "v", 0, 3), ("b", "v", 0, 3), ("d", "v", 3, 7), ("c", "v", 13, 16, "B1"),
-        ("b", "v", 3, 7), ("d", "v", 7, 10), ("d", "v", 10, 12), ("b", "v", 7, 10), ("d", "v", 12, 13),
-        ("l", "v", 12, 13), ("b", "v", 10, 12), ("r", "v", 12, 13), ("f", 4)]
+        ("d", "y", 0, 4), ("d", "y", 4, 8), ("d", "y", 8, 12), ("d", "y", 12, 14), ("i", "v", 0),
+        ("d", "y", 14, 15), ("i", "v", 1), ("d", "y", 15, 16), ("i", "v", 2), ("f", 3),
+        ("b", "y", 0, 4), ("b", "y", 4, 8), ("b", "y", 8, 12), ("preQ",), ("b", "y", 12, 16),
+        ("d", "v", 0, 3), ("g", "v", 13, 16, "B1"), ("b", "v", 0, 3), ("d", "v", 3, 6), ("b", "v", 3, 6),
+        ("d", "v", 6, 8), ("b", "v", 6, 8), ("d", "v", 8, 11), ("c", "v", 13, 16, "B1"), ("d", "v", 11, 13),
+        ("l", "v", 11, 13), ("b", "v", 8, 11), ("t", "SGa"), ("r", "v", 11, 13)]
 MAG = 12582912.0
 MAG11 = 1.5 * 2.0 ** 34
 
@@ -37,10 +43,13 @@ _decl("ZB ZR ONESB IB NIB I2B I4K IN2K GX GD CT MM YZ", 128, "bfloat16")
 _decl("Z2 WM J16 C1 C2A C2B I16", 128, "float16")
 _decl("G KP GEP D0 C128 I32 NI32 ZZ FU SG S1 S2 RQ RC QO FS TQ", 128, "float32")
 _decl("GE", 144, "float32")
-_decl("EBP EBN EB2P EB2N WE", 144, "bfloat16")
+_decl("EBP EBN EB2P EB2N", 144, "bfloat16")
+_decl("WB MKD NE", 128, "bfloat16")
+_decl("RS SU", 128, "float32")
+_decl("F16 T2 P8", 8, "float32")
 _decl("IX IY IV", 128, "uint16")
 _decl("PERM OI OE OC OC0 CL OR OP", 8, "uint16")
-_decl("K A1 A2 S CD KI A15 A511 A3", 8, "int32")
+_decl("K A1 A2 S CD KI A511 A3", 8, "int32")
 _decl("B8 BT BP BOFF AT NB AP CJ", 8, "float32")
 _decl("NN", 8, "bfloat16")
 _decl("LE", 16, "float32")
@@ -55,7 +64,7 @@ STORES = ["yc", "yp", "yq", "yl", "yx", "yz"]
 SEMAPHORES = (["sv", "sa", "sp", "sg", "ls"] + ["l_" + n for n in LOADS] + ["o_" + n for n in STORES]
               + ["m%d" % i for i in range(VIS)])
 
-PF, KF, G16, T7, PB, C37, CA, CE, C16, WF, WH, CTHR, THR, CNT, CB1, CF1, CF2 = range(17)
+PF, KF, G16, T7, PB, C37, CA, CE, CE1, C16, WF, WH, CTHR, THR, CNT, CB1, CF1, CF2 = range(18)
 
 
 def message(T, i):
@@ -255,18 +264,19 @@ def rank_program(g, core, T, topo):
     load("s", "pa", R("PI_"))
     load("s", "vi", R("QI"))
     load("s", "de", R("DI", 0, 1))
-    load("s", "pl", R("PLI"))
+    op("s", lambda: g.sync.dma_start(ap(R("PLI")), T.pl[:]), [R("TAB")], [R("PLI")], "l_pl", 16)
     iota(R("PN"), [[0, 1]], 0, 1, False)
     iota(R("G"), [[16, 8], [0, 16]], 0, 0)
     iota(R("B8"), [[1, 8]], 0, 0)
     iota(R("GE"), [[1, 144]], -16, 0)
     iota(R("KP"), [[0, 8], [1, 16]], 0, 0)
+    iota(R("P8"), [[64, 2], [4, 4]], 0, 0)
     iota(R("MK"), [[0, 2048]], 1, 0)
     mset(R("CUT"), 0.0)
     ts(R("KN"), R("PN"), 15, A.bitwise_and)
     cp(col(PF), R("PN"))
     cp(col(KF), R("KN"))
-    ts(R("R7"), R("PN"), 7, A.bitwise_and)
+    ts(R("R7"), R("PN"), 3, A.bitwise_and)
     tt(col(G16), col(PF), col(KF), A.subtract)
     ts(R("GEP", 0, 16), R("KP", 0, 16), col(KF), A.is_le)
     ts(R("LE"), R("KP", 0, 16), col(KF), A.add, 15.0, A.is_le)
@@ -274,24 +284,27 @@ def rank_program(g, core, T, topo):
     ts(R("C2B"), R("G"), 0.0, A.mult, 2.0, A.add)
     ts(R("J16"), R("G"), col(G16), A.is_equal)
     ts(R("I32"), R("GE", 16, 144), col(PF), A.is_equal)
-    ts(R("R8"), R("PN"), 3, A.logical_shift_right, 1, A.bitwise_and)
+    ts(R("R8"), R("PN"), 2, A.logical_shift_right, 3, A.bitwise_and)
     ts(col(T7), R("R7"), 16.0, A.mult)
     ts(R("EBP"), R("GE"), col(G16), A.is_equal, 16384.0, A.mult)
+    ts(R("NE"), R("KP"), col(KF), A.not_equal)
     ts(col(WH), R("WI", 0, 1), 0.5, A.mult)
     ts(R("Z2"), R("ZB"), 2.0, A.mult)
     ts(R("WM"), R("G"), col(G16), A.is_equal, col(WH), A.mult)
     tt(col(PB), col(T7), R("R8"), A.add)
     cp(C_(0), R("CI"))
     ts(col(C37), col(KF), 37.0, A.mult)
-    ts(R("PERM"), R("B8"), 2.0, A.mult, col(PB), A.add)
+    ts(R("PERM"), R("P8"), col(PB), A.add)
 
-    act(col(CA), col(KF), scale=128.0)
-    act(col(CE), col(KF), scale=128.0, bias=127.0)
+    act(col(CA), col(KF), scale=64.0)
+    act(col(CE), col(KF), scale=64.0, bias=127.0)
+    act(col(CE1), col(KF), scale=64.0, bias=63.0)
     act(col(C16), col(KF), scale=16.0)
     act(R("BOFF"), R("B8"), scale=524288.0)
     act(R("D0"), R("G"), scale=32641.0, bias=30720.0)
     act(R("BT"), R("B8"), scale=256.0, bias=col(C16))
     act(R("BP"), R("BT"), scale=0.25)
+    act(R("BT"), R("BT"), bias=7.5)
     for e1 in range(16):
         act(R("CUT", 128 * e1, 128 * e1 + 16), R("GEP", 0, 16), F.Copy, scale=R("LE", e1, e1 + 1))
     act(R("NI32"), R("I32"), scale=-1.0)
@@ -310,6 +323,7 @@ def rank_program(g, core, T, topo):
     act(R("I4K"), R("I32"), scale=4096.0)
     act(R("IN2K"), R("I32"), scale=-2048.0)
     act(R("ZZ"), R("ZB"), bias=2047.5)
+    act(R("MKD"), R("NE"), scale=-4194304.0, bias=-7.5)
 
     def u_pre():
         mm(U1, R("J16"), R("C2A"), True, False)
@@ -325,10 +339,6 @@ def rank_program(g, core, T, topo):
         return [lambda: tt(R("H" + s), U2, n, A.mult),
                 lambda: ts(R("G" + s), R("H" + s), 5, A.logical_shift_right, 2047, A.bitwise_and),
                 lambda: ts(R("I" + s.upper()), (R("G" + s), R("PERM")), col(C37), A.add)]
-
-    def u_mod():
-        ts(R("FU"), U1, MAG11, A.add, MAG11, A.subtract)
-        tt(U2, U2, R("FU"), A.subtract)
 
     def weave(*chains):
         k = max(len(c) for c in chains)
@@ -349,14 +359,21 @@ def rank_program(g, core, T, topo):
            lambda: cp(R("EAR", 128, 256), R("QI")),
            lambda: mset(R("ONESB"), 1.0)])
     late = [lambda: ts(R("I16"), R("GE", 16, 144), col(PF), A.is_equal),
-            lambda: ts(R("WE"), R("GE"), col(G16), A.is_equal, col(WF), A.mult),
+            lambda: ts(R("WB"), R("G"), col(G16), A.is_equal, col(WF), A.mult),
             lambda: ts(R("C1"), R("G"), 0.0, A.mult, -2048.0, A.add),
-            lambda: mset(R("C128"), 128.0)]
+            lambda: mset(R("C128"), 128.0),
+            lambda: ts(R("RS"), R("KP"), 0.0, A.is_equal, -8388608.0, A.mult)]
 
-    def dmm(a, buf, eb, start, stop):
-        mm(R("B0", 0, 128), R(eb, 16 - a, 144 - a), R(buf, 128 * a, 128 * a + 128), start, stop)
+    dbank = ("B7", "B0")
 
-    n_dmm = sum(tk[3] - tk[2] for tk in PLAN if tk[0] in ("l", "r", "b", "c"))
+    def dmm(j, buf, eb, start, stop):
+        for s_ in range(2):
+            a = 2 * (j % 8) + s_
+            mm(R(dbank[j // 8], 0, 64), R(eb, 16 - a, 144 - a), R(buf, 128 * j + 64 * s_, 128 * j + 64 * s_ + 64),
+               start and s_ == 0, stop and s_ == 1)
+
+    n_dmm = [sum(1 for tk in PLAN if tk[0] in ("l", "r", "b", "c") for j in range(tk[2], tk[3]) if j // 8 == h)
+             for h in range(2)]
     plain_v = [a for tk in PLAN if tk[0] == "g" and tk[1] == "v" for a in range(tk[2], tk[3])]
 
     for t in range(VIS):
@@ -376,16 +393,44 @@ def rank_program(g, core, T, topo):
                     lambda: tt(R("AP"), R("A3"), R("NB"), A.add),
                     lambda: cp(R("OP"), R("AP")),
                     lambda: cp((R("POOL"), R("OP")), C_(t))]
-        done = [0]
+        done = [0, 0]
 
-        def dsum(a, buf, eb):
-            dmm(a, buf, eb, done[0] == 0, done[0] == n_dmm - 1)
-            done[0] += 1
+        def dsum(j, buf, eb):
+            h = j // 8
+            dmm(j, buf, eb, done[h] == 0, done[h] == n_dmm[h] - 1)
+            done[h] += 1
+
+        def half(h):
+            c0, c1, b0, b1, x0, x1 = 64 * h, 64 * h + 64, 4 * h, 4 * h + 4, 1024 * h, 1024 * h + 1024
+            oi, oe = R("OI", b0, b1), R("OE", b0, b1)
+            return {
+                "SG": lambda: ts(R("SG", c0, c1), R(dbank[h], 0, 64), -16384.0, A.max, 16384.0, A.min),
+                "S1": lambda: scan(R("S1", c0, c1), R("D0", c0, c1), R("SG", c0, c1), 0.0, A.max, A.subtract),
+                "S2": lambda: scan(R("S2", c0, c1), R("C128", c0, c1), R("S1", c0, c1), 0.0, A.add, A.max),
+                "K": lambda: tt(R("K", b0, b1), R("S2", c0 + 15, c1, 16), R("BOFF", b0, b1), A.subtract),
+                "A1": lambda: ts(R("A1", b0, b1), R("K", b0, b1), 127, A.bitwise_and),
+                "OI": lambda: ts(oi, R("A1", b0, b1), col(CA), A.add, -64.0 * h, A.add),
+                "A2": lambda: ts(R("A2", b0, b1), R("K", b0, b1), 7, A.logical_shift_right, 127, A.bitwise_and),
+                "OE": lambda: ts(oe, R("A2", b0, b1), -1.0, A.mult, col(CE + h), A.add),
+                "MK": lambda: cp((R("MK", x0, x1), oi), R("ZR", 0, 64)),
+                "SC": lambda: scan(R("SC", x0, x1), R("MK", x0, x1), R("X", x0, x1), 0.0, A.mult, A.max),
+                "GX": lambda: act(R("GX", c0, c1), (R("X", x0, x1), oi), F.Copy),
+                "GD": lambda: act(R("GD", c0, c1), (R("DV", x0, x1), oi), F.Copy),
+                "MM": lambda: act(R("MM", c0, c1), (R("SC", x0, x1), oe), F.Copy),
+                "Z2": lambda: tt(R("Z2", c0, c1), (R("SC", x0, x1), oe), R("ZZ", c0, c1), A.add),
+            }
+
+        halves = {}
+        for h in range(2):
+            for nm, fn in half(h).items():
+                halves[nm + "ab"[h]] = fn
 
         for tk in PLAN:
             kind = tk[0]
             if kind == "f":
                 fill[tk[1]]()
+            elif kind == "t":
+                halves[tk[1]]()
             elif kind == "i":
                 if t == 1 and tk[1:] == ("v", 0):
                     tt(R("TQ"), (R("CUT"), R("CL")), R("EL", 0, 128), A.mult)
@@ -395,6 +440,7 @@ def rank_program(g, core, T, topo):
                     late[tk[2]]()
                     if tk[2] == 2:
                         late[3]()
+                        late[4]()
             elif kind == "preC":
                 mm(R("B5", 0, 128), R("I32"), P_(t), True, False)
                 mm(R("B5", 0, 128), R("NI32"), C_(t), False, False)
@@ -413,6 +459,8 @@ def rank_program(g, core, T, topo):
                 one, two, lin = ("EBN", "EB2N", "EBP") if s_ == "y" else ("EBP", "EB2P", "EBN")
                 if kind == "X":
                     act(R("X", lo, hi), lst, F.Copy)
+                elif kind == "W":
+                    cp(R("X", lo, hi), lst)
                 elif kind == "d":
                     tt(R(dd, lo, hi), lst, R("X", lo, hi), A.subtract)
                 elif kind == "l":
@@ -438,101 +486,112 @@ def rank_program(g, core, T, topo):
             u_pre()
         oc = R("OC0") if t == 0 else R("OC")
         thr = col(CTHR) if t == 0 else col(THR)
-        ts(R("SG"), R("B0", 0, 128), -16384.0, A.max, 16384.0, A.min)
-        scan(R("S1"), R("D0"), R("SG"), 0.0, A.max, A.subtract)
-        scan(R("S2"), R("C128"), R("S1"), 0.0, A.add, A.max)
-        tt(R("K"), R("S2", 15, 128, 16), R("BOFF"), A.subtract)
-        ts(R("A1"), R("K"), 127, A.bitwise_and)
-        ts(R("S"), R("K"), thr, A.subtract, -1.0, A.max)
-        ts(R("OI"), R("A1"), col(CA), A.add)
-        ts(R("CD"), R("S"), 0x78F, A.bitwise_and)
-        ts(R("A2"), R("K"), 7, A.logical_shift_right, 127, A.bitwise_and)
-        cp(oc, R("CD"))
-        cp((R("MK"), R("OI")), R("ZR"))
-        ts(R("OE"), R("A2"), -1.0, A.mult, col(CE), A.add)
-        scan(R("SC"), R("MK"), R("X"), 0.0, A.mult, A.max)
-        if t == 0:
-            send(1)
-        act(R("CT"), (R("CUT"), oc), F.Copy)
-        if qsel:
-            mm(R("B3", 0, 128), R("I4K"), R("CT"), False, True)
-        mm(R("B5", 0, 128), R("I4K"), R("CT"), False, True)
-        if qsel:
-            mm(R("B4", 0, 128), R("IN2K"), R("CT"), False, False)
-        mm(R("B6", 0, 128), R("IN2K"), R("CT"), False, False)
-        act(R("GX"), (R("X"), R("OI")), F.Copy)
-        if qsel:
-            act(R("RQ"), R("B3", 0, 128), F.Relu, bias=-2048.0)
-            mm(R("B4", 0, 128), R("I32"), R("RQ"), False, True)
-        act(R("RC"), R("B5", 0, 128), F.Relu, bias=-2048.0)
-        mm(R("B6", 0, 128), R("I32"), R("RC"), False, True)
-        act(R("GD"), (R("DV"), R("OI")), F.Copy)
-        mm(R("B7", 0, 128), R("I2B"), R("GX"), True, False)
-        for a in plain_v:
-            mm(R("B7", a, 128, 16), R("NIB"), R("GX", a, 128, 16), False, False)
-        mm(R("B7", 0, 128), R("IB"), R("GD"), False, True)
-        if qsel:
+        um = R("SU", 15, 128, 16)
+        x3 = idx_steps(C_(t + 1), "x")
+
+        def m_s():
+            mm(R("B7", 0, 128), R("I2B"), R("GX"), True, False)
+            for j in plain_v:
+                for a in (2 * (j % 8), 2 * (j % 8) + 1):
+                    lanes = (64 * (j // 8) + a, 64 * (j // 8) + 64, 16)
+                    mm(R("B7", *lanes), R("NIB"), R("GX", *lanes), False, False)
+            mm(R("B7", 0, 128), R("IB"), R("GD"), False, True)
+
+        def new_q():
             act(R("QO"), R("B4", 0, 128), F.Copy)
             if last:
                 store("s", "yq", R("QO"))
             else:
                 send(t + 1)
-        act(C_(t + 1), R("B6", 0, 128), F.Copy)
-        if last:
-            store("s", "yc", C_(t + 1))
-        else:
-            iota(R("MK"), [[0, 2048]], 1, 0)
-        act(R("MM"), (R("SC"), R("OE")), F.Copy)
-        tt(R("Z2"), (R("SC"), R("OE")), R("ZZ"), A.add)
-        ts(R("NN"), R("S"), 0.0, A.is_lt, 512.0, A.mult)
-        act(R("FS"), R("B7", 0, 128), scale=0.4995, bias=MAG)
-        act(R("VAL", 0, 128), R("FS"), bias=-MAG)
-        if not last:
-            act(R("VAL", 128, 176), R("FS", 0, 48), bias=-MAG)
-            u_main()
-        for a in range(16):
-            mm(R("B0", 0, 8), R("WE", 16 - a, 144 - a), R("MM", a, 128, 16), a == 0, a == 15)
-        mm(R("B7", 0, 128), R("I16"), R("Z2"), True, True)
-        tab = [lambda: cp(R("KI"), R("B0", 0, 8)),
-               lambda: ts(R("A15"), R("KI"), 15, A.bitwise_and),
-               lambda: ts(R("A511"), R("KI"), 511, A.bitwise_and),
-               lambda: tt(R("AT"), R("A15"), R("BT"), A.add),
-               lambda: cp(R("OR"), R("A511")),
-               lambda: cp(R("OT", 0, 8), R("AT")),
-               lambda: cp((R("TAB"), R("OT", 0, 8 if last else 11)), R("VAL", 0, 128 if last else 176)),
-               lambda: ts(R("OT", 8, 11), R("AT", 0, 3), 2048.0, A.add)]
-        if not last:
-            u_mod()
-            x4 = idx_steps(C_(t + 1), "x")
-            for (w_, i_) in TAIL:
-                (x4 if w_ == "x" else tab)[i_]()
-            act(R("ZZ"), R("B7", 0, 128), scale=0.5, bias=1023.5)
-            mm(R("B7", 0, 8), R("ONESB"), R("NN"), True, True)
+
+        def code():
+            cp(oc, R("CD"))
+            if t == 0:
+                send(1)
+
+        def new_c():
+            act(C_(t + 1), R("B6", 0, 128), F.Copy)
+            if last:
+                store("s", "yc", C_(t + 1))
+
+        def new_table():
+            cp((R("TAB"), R("OT", 0, 8 if last else 11)), R("VAL", 0, 128 if last else 176))
+            if last:
+                store("s", "yx", R("TAB", 0, 2048))
+
+        def new_marks():
+            if last:
+                act(R("YZ"), R("B7", 0, 128), scale=0.5, bias=-1024.0)
+                store("a", "yz", R("YZ"))
+            else:
+                act(R("ZZ"), R("B7", 0, 128), scale=0.5, bias=1023.5)
+
+        def new_p():
             act(P_(t + 1), (R("POOL", 0, 512), R("OR")), F.Copy)
-            act(R("CJ"), R("B7", 0, 8), scale=1.0 / 512, accum=col(CNT))
-            act(col(CF1), col(CNT), scale=0.4999, bias=MAG)
-            act(col(CB1), col(CNT), scale=16384.0, bias=col(CTHR))
-            act(col(CF2), col(CF1), bias=-MAG)
-            act(col(THR), col(CF2), scale=-32768.0, bias=col(CB1))
-        else:
-            tt(R("NB"), R("NN"), R("BP"), A.add)
-            tab[0]()
-            tab[1]()
-            tab[2]()
-            tab[3]()
-            tab[4]()
-            tab[5]()
-            ts(R("A3"), R("KI"), 3, A.bitwise_and)
-            tab[6]()
-            store("s", "yx", R("TAB", 0, 2048))
-            tt(R("AP"), R("A3"), R("NB"), A.add)
-            cp(R("OP"), R("AP"))
-            act(R("YZ"), R("B7", 0, 128), scale=0.5, bias=-1024.0)
-            act(P_(t + 1), (R("POOL", 0, 512), R("OR")), F.Copy)
+            if last:
+                store("a", "yp", P_(t + 1))
+
+        def new_pool():
             cp((R("POOL"), R("OP")), C_(t + 1))
-            store("a", "yz", R("YZ"))
-            store("a", "yp", P_(t + 1))
             store("a", "yl", R("POOL", 0, 512))
+
+        step = {
+            "S": lambda: ts(R("S"), R("K"), thr, A.subtract, -1.0, A.max),
+            "CD": lambda: ts(R("CD"), R("S"), 0x78F, A.bitwise_and),
+            "OC": code,
+            "PS": fill[4],
+            "NN": lambda: ts(R("NN"), R("S"), 0.0, A.is_lt, 512.0, A.mult),
+            "CT": lambda: act(R("CT"), (R("CUT"), oc), F.Copy),
+            "mQ1": lambda: mm(R("B3", 0, 128), R("I4K"), R("CT"), False, True),
+            "mQ2": lambda: mm(R("B4", 0, 128), R("IN2K"), R("CT"), False, False),
+            "mC1": lambda: mm(R("B5", 0, 128), R("I4K"), R("CT"), False, True),
+            "mC2": lambda: mm(R("B6", 0, 128), R("IN2K"), R("CT"), False, False),
+            "RQ": lambda: act(R("RQ"), R("B3", 0, 128), F.Relu, bias=-2048.0),
+            "RC": lambda: act(R("RC"), R("B5", 0, 128), F.Relu, bias=-2048.0),
+            "mQ3": lambda: mm(R("B4", 0, 128), R("I32"), R("RQ"), False, True),
+            "mC3": lambda: mm(R("B6", 0, 128), R("I32"), R("RC"), False, True),
+            "QO": new_q,
+            "CN": new_c,
+            "mS": m_s,
+            "FS": lambda: act(R("FS"), R("B7", 0, 128), scale=0.4995, bias=MAG),
+            "VAL": lambda: act(R("VAL", 0, 128), R("FS"), bias=-MAG),
+            "VAL2": lambda: act(R("VAL", 128, 176), R("FS", 0, 48), bias=-MAG),
+            "IO": lambda: iota(R("MK"), [[0, 2048]], 1, 0),
+            "mU": u_main,
+            "mM0": lambda: mm(R("B0", 0, 128), R("IB"), R("MKD"), True, False),
+            "mM": lambda: mm(R("B0", 0, 128), R("WB"), R("MM"), False, True),
+            "SU": lambda: scan(R("SU"), R("RS"), R("B0", 0, 128), -8388608.0, A.add, A.max),
+            "F16": lambda: ts(R("F16"), um, MAG4, A.add, MAG4, A.subtract),
+            "T2": lambda: tt(R("T2"), um, R("BT"), A.add),
+            "AT": lambda: tt(R("AT"), R("T2"), R("F16"), A.subtract),
+            "OT": lambda: cp(R("OT", 0, 8), R("AT")),
+            "OT2": lambda: ts(R("OT", 8, 11), R("AT", 0, 3), 2048.0, A.add),
+            "TAB": new_table,
+            "KI": lambda: ts(R("KI"), um, 7.5, A.add),
+            "A511": lambda: ts(R("A511"), R("KI"), 511, A.bitwise_and),
+            "OR": lambda: cp(R("OR"), R("A511")),
+            "PN": new_p,
+            "FU": lambda: ts(R("FU"), U1, MAG11, A.add, MAG11, A.subtract),
+            "UU": lambda: tt(U2, U2, R("FU"), A.subtract),
+            "x0": x3[0], "x1": x3[1], "x2": x3[2],
+            "mZ": lambda: mm(R("B7", 0, 128), R("I16"), R("Z2"), True, True),
+            "ZZ": new_marks,
+            "mN": lambda: mm(R("B5", 0, 8), R("ONESB"), R("NN"), True, True),
+            "CJ": lambda: act(R("CJ"), R("B5", 0, 8), scale=1.0 / 512, accum=col(CNT)),
+            "c1": lambda: act(col(CF1), col(CNT), scale=0.4999, bias=MAG),
+            "c2": lambda: act(col(CB1), col(CNT), scale=16384.0, bias=col(CTHR)),
+            "c3": lambda: act(col(CF2), col(CF1), bias=-MAG),
+            "c4": lambda: act(col(THR), col(CF2), scale=-32768.0, bias=col(CB1)),
+            "A3": lambda: ts(R("A3"), R("KI"), 3, A.bitwise_and),
+            "NB": lambda: tt(R("NB"), R("NN"), R("BP"), A.add),
+            "AP": lambda: tt(R("AP"), R("A3"), R("NB"), A.add),
+            "OP": lambda: cp(R("OP"), R("AP")),
+            "PL": new_pool,
+        }
+        step.update(halves)
+        for nm in (CUTS + " " + (LAST if last else TAIL)).split():
+            if qsel or nm not in ("mQ1", "mQ2", "RQ", "mQ3", "QO"):
+                step[nm]()
 
     for s in sorted(cnt):
         g.wait_ge(T.sem[s], cnt[s])

@@ -4,25 +4,33 @@ from concourse.mybir import dt, AluOpType, AxisListType, ActivationFunctionType
 A = AluOpType
 F = ActivationFunctionType
 VIS = 6
-MAG4 = 1.5 * 2.0 ** 27
-CUTS = ("S1a S2a SGb mM0 Ka S1b A1a A2a S2b OIa OEa Kb MKa S A1b A2b CD OIb OEb OC MKb SCa SCb Z2a "
-        "GXa GDa CT mQ1 mQ2 mC1 mC2 GXb RQ MMa")
-TAIL = ("mQ3 RC MMb Z2b mU mM QO IO PS mC3 GDb mS CN FS VAL VAL2 "
-        "FU SU NN UU mN F16 T2 KI x0 AT A511 x1 OT OT2 OR x2 TAB mZ CJ c1 c2 c3 PN c4 ZZ")
-LAST = ("RC GDb mS MMb PS NN Z2b NB mM mQ3 mC3 FS VAL CN QO mZ "
-        "SU F16 T2 KI AT A511 A3 OT OR ZZ AP TAB OP PN PL")
-PLAN = [("X", "x", 0, 4), ("X", "x", 4, 8), ("X", "x", 8, 12), ("X", "x", 12, 16), ("preC",),
-        ("i", "y", 0), ("f", 0), ("i", "y", 1), ("f", 1), ("i", "y", 2), ("f", 2),
-        ("d", "y", 0, 4), ("d", "y", 4, 8), ("d", "y", 8, 12), ("d", "y", 12, 14), ("i", "v", 0),
-        ("d", "y", 14, 15), ("i", "v", 1), ("d", "y", 15, 16), ("i", "v", 2), ("f", 3),
-        ("b", "y", 0, 4), ("b", "y", 4, 8), ("b", "y", 8, 12), ("preQ",), ("b", "y", 12, 16),
-        ("d", "v", 0, 3), ("g", "v", 13, 16, "B1"), ("b", "v", 0, 3), ("d", "v", 3, 6), ("b", "v", 3, 6),
-        ("d", "v", 6, 8), ("b", "v", 6, 8), ("d", "v", 8, 11), ("c", "v", 13, 16, "B1"), ("d", "v", 11, 13),
-        ("l", "v", 11, 13), ("b", "v", 8, 11), ("t", "SGa"), ("r", "v", 11, 13)]
+EXT = 560
 MAG = 12582912.0
-MAG11 = 1.5 * 2.0 ** 34
+LIFT = 1056.0
+NBS = (4, 4)
+PLAN = ([("x", "a", 0, 9), ("x", "v", 9, 16), ("y", "S", 0, 8), ("y", "S", 8, 15), ("y", "M", 15, 16),
+         ("v", "V", 0, 8), ("v", "V", 8, 16)],
+        [("x", "a", 0, 8), ("x", "a", 8, 16), ("y", "S", 0, 8), ("y", "S", 8, 16),
+         ("v", "V", 0, 3), ("v", "M", 3, 8), ("v", "V", 8, 10), ("v", "V", 10, 16)])
+RANK = {"lx": (-77, -76), "ly": (-112, -47), "lv": (-35, -95), "x": (-30, 16), "y": (6, 22), "v": (-15, 69),
+        "cut": (-92, 13), "rec": (35, 16), "max": (80, -4), "place": (4, 43), "val": (122, 53), "tab": (248, -5),
+        "mark": (-89, 19), "pool": (160, 108), "count": (92,), "child": (38, 53)}
+QUICK = (True, False)
+LAST = {"x": (-33, 8), "y": (-24, 33), "v": (-33, 65), "pool": (140, 100), "mark": (38, 93), "max": (25, -33),
+        "place": (36, 1), "val": (33, 43), "tab": (18, 49), "cut": (-68, -2), "rec": (11, 33)}
+CY, WAKE, GATHER, SCATTER, PECY, DMA0, DMAB, HOP, SLACK = 0.00087, 0.15, 1.3, 2.8, 0.00048, 1.6, 0.00032, 3.75, 0.03
+NEAR, ROWS = 0.15, 0.4
+ON = dict([(n, "v") for n in "NNb Iva Ivb OOa OCa DQa GDa CFa".split()]
+          + [(n, "a") for n in "Ixa Ixb Iya Iyb OOb OCb CTb KCa GXb GDb VALa VALb MMb Pa Pb Za FUa FUb CFa1".split()])
+FIRST = {"lx": (-75, -59), "ly": (-77, -26), "lv": (-56, -24), "x": (-58, -52), "y": (-43, 25), "v": (16, 85),
+         "rec": (49, 28)}
+LATER = -0.5
+CH = range(len(NBS))
+INHERIT = False
+LONG, SOON, FIT, PIECES = 0.15, 0.07, 0.03, (1, 1)
 
 SCRATCH = {}
+SIZE = {"float32": 4, "int32": 4, "bfloat16": 2, "float16": 2, "uint16": 2}
 
 
 def _decl(names, cols, dtype, where="sbuf"):
@@ -32,47 +40,50 @@ def _decl(names, cols, dtype, where="sbuf"):
 
 _decl("X DV DY AV AY SC MK CUT", 2048, "bfloat16")
 _decl("TAB", 2048 + 768, "bfloat16")
-_decl("VAL", 176, "bfloat16")
-_decl("OT", 12, "uint16")
-_decl("POOL", 1024, "float32")
+_decl("POOL POOL2", 1536, "float32")
 _decl("PLI", 512, "int32")
-_decl("S30 S31 S32 S33 S34 S35 S36", 384, "float32")
-_decl("EAR EL", 256, "float32")
-_decl("CI PI_ QI Hx Hy Hv Gx Gy Gv", 128, "int32")
-_decl("ZB ZR ONESB IB NIB I2B I4K IN2K GX GD CT MM YZ", 128, "bfloat16")
-_decl("Z2 WM J16 C1 C2A C2B I16", 128, "float16")
-_decl("G KP GEP D0 C128 I32 NI32 ZZ FU SG S1 S2 RQ RC QO FS TQ", 128, "float32")
+_decl("S1_ S2_ S3_ S4_ S5_", 384, "float16")
+_decl("S6_", 384, "float32")
+_decl("V1 V2 V3 V4 V5 P0 FU I16 NI16 IH16 N2K CN Z WS W16 WN DQ TQ", 128, "float16")
+_decl("EAR EL KEEP", 256, "float16")
+_decl("CI PI_ QI Hx Hy Hv Gx Gy Gv VAL SU", 128, "int32")
+_decl("ZB ZR IB NIB IH NIH I4K N4K GX GD CT CTV MM WB MKD C32 ONE", 128, "bfloat16")
+_decl("G KP D0 C128 SG S1 S2 RS", 128, "float32")
 _decl("GE", 144, "float32")
 _decl("EBP EBN EB2P EB2N", 144, "bfloat16")
-_decl("WB MKD NE", 128, "bfloat16")
-_decl("RS SU", 128, "float32")
-_decl("F16 T2 P8", 8, "float32")
-_decl("IX IY IV", 128, "uint16")
-_decl("PERM OI OE OC OC0 CL OR OP", 8, "uint16")
-_decl("K A1 A2 S CD KI A511 A3", 8, "int32")
-_decl("B8 BT BP BOFF AT NB AP CJ", 8, "float32")
+_decl("Ix Iy Iv", 128, "uint16")
+_decl("PERM0 PERM1 OC0 OC1 OD0 OD1 CL0 CL1", 8, "uint16")
+_decl("OO0 OO1", 16, "uint16")
+_decl("OL0 OL1", 24, "uint16")
+_decl("KK0 KK1 AA0 AA1", 16, "int32")
+_decl("AT0 AT1", 24, "int32")
+_decl("OFF0 OFF1", 24, "float16")
+_decl("CD PA", 8, "int32")
+_decl("B8 BOFF BT PW", 8, "float32")
 _decl("NN", 8, "bfloat16")
-_decl("LE", 16, "float32")
+_decl("LE GEP", 16, "float32")
 _decl("WI DI", 4, "int32")
-_decl("PN KN R7 R8", 1, "int32")
+_decl("PN", 2, "int32")
 _decl("CF", 24, "float32")
-_decl("B0 B1 B2 B3 B4 B5 B6 B7", 512, "float32", "psum")
+_decl("BD0 BD1 BF0 BF1 BG1 BG2 BU0 BU1", 512, "float32", "psum")
 
-EXT = 560
 LOADS = ["wt", "zt", "ch", "pa", "de", "vi", "pl", "xt", "x2"]
-STORES = ["yc", "yp", "yq", "yl", "yx", "yz"]
-SEMAPHORES = (["sv", "sa", "sp", "sg", "ls"] + ["l_" + n for n in LOADS] + ["o_" + n for n in STORES]
-              + ["m%d" % i for i in range(VIS)])
+NMSG = 1 + len(NBS) * (VIS - 1)
+SEMAPHORES = ["sv", "sa", "sp", "sg", "ls", "out"] + ["l_" + n for n in LOADS] + ["m%d" % i for i in range(NMSG)]
 
-PF, KF, G16, T7, PB, C37, CA, CE, CE1, C16, WF, WH, CTHR, THR, CNT, CB1, CF1, CF2 = range(18)
+PF, KF, G16, C37, C16, C4, WF, WG, CTHR, THR, CF1, CF2, UB, C4P, CA = range(15)
+B0 = (0, NBS[0])
+LANES = [(16 * B0[h], 16 * (B0[h] + NBS[h])) for h in CH]
 
 
-def message(T, i):
+def message(i):
     if i == 0:
         return ("EAR", 0, 256), ("EL", 0, 256)
-    if i == 1:
-        return ("OC0", 0, 8), ("CL", 0, 8)
-    return ("QO", 0, 128), ("S3%d" % i, 256, 384)
+    t, h = divmod(i - 1, len(NBS))
+    c0, c1 = LANES[h]
+    if t == 0:
+        return ("OD%d" % h, 0, 8), ("CL%d" % h, 0, 8)
+    return ("S%d_" % (t + 1), 3 * c0, 2 * c0 + c1), ("V%d" % (t + 1), c0, c1)
 
 
 def route(T, topo, r):
@@ -85,15 +96,587 @@ def route(T, topo, r):
     return [src, (near or cand)[0], dst]
 
 
+def R(n, lo=0, hi=None, st=None):
+    if hi is None:
+        hi = SCRATCH[n][1][1]
+    return (n, lo, hi) if st is None else (n, lo, hi, st)
+
+
+def col(c):
+    return ("CF", c, c + 1)
+
+
+def width(r):
+    if isinstance(r[0], tuple):
+        return 16 * width(r[1])
+    return len(range(*r[1:]))
+
+
+def program():
+    calls = []
+    rank = [-10000]
+
+    def stage(name, t, h=0):
+        rank[0] = 100 * t + {0: FIRST, VIS - 1: LAST}.get(t, {}).get(name, RANK[name])[h]
+        now[:] = [t, h]
+
+    now, label, met = [], [], {}
+
+    def tag(out):
+        if not now:
+            return None
+        base = (label.pop() if label else (out[0][0] if isinstance(out[0], tuple) else out[0]).rstrip("01")) + "ab"[now[1]]
+        k = met[now[0], base] = met.get((now[0], base), -1) + 1
+        return now[0], base + (str(k) if k else "")
+
+    def put(e, kind, args, outs, ins, cost, after=()):
+        rd, wr = [], []
+        for x in ins:
+            if isinstance(x, tuple):
+                rd += [x[0][:3], x[1][:3]] if isinstance(x[0], tuple) else [x[:3]]
+        for x in outs:
+            if isinstance(x[0], tuple):
+                wr.append(x[0][:3])
+                rd.append(x[1][:3])
+            else:
+                wr.append(x[:3])
+        calls.append((e, kind, args, rd, wr, cost, list(after), rank[0], tag(outs[0]) if e in "vaf" and outs else None))
+        return len(calls) - 1
+
+    def cyc(out, ins, rate=1.0):
+        if isinstance(out[0], tuple):
+            return 0.05 + SCATTER * width(out) * CY
+        if isinstance(ins[0][0], tuple):
+            return 0.06 + GATHER * width(out) * CY
+        return 0.06 + rate * width(out) * CY
+
+    def fast(*x):
+        return 0.5 if all(not isinstance(r[0], tuple) and SIZE[SCRATCH[r[0]][2]] == 2 for r in x) else 1.0
+
+    def cp(out, in_):
+        put("v", "cp", (out, in_), [out], [in_], cyc(out, [in_], fast(out, in_)))
+
+    def tt(out, a, b, alu):
+        both = not isinstance(a[0], tuple) and SCRATCH[a[0]][0] == SCRATCH[b[0]][0]
+        put("v", "tt", (out, a, b, alu), [out], [a, b], cyc(out, [a], 2.0 if both else 1.0))
+
+    def ts(out, a, s1, o0, s2=None, o1=None):
+        put("v", "ts", (out, a, s1, s2, o0, o1), [out], [a, s1, s2], cyc(out, [a], fast(out, a)))
+
+    def scan(out, d0, d1, init, o0, o1):
+        put("v", "scan", (out, d0, d1, init, o0, o1), [out], [d0, d1], cyc(out, [d0], fast(out, d0, d1)))
+
+    def mset(out, v):
+        put("v", "mset", (out, v), [out], [], cyc(out, [out], fast(out)))
+
+    def act(out, in_, func=F.Identity, bias=0.0, scale=1.0):
+        put("a", "act", (out, in_, func, bias, scale), [out], [in_, bias, scale], cyc(out, [in_]))
+
+    def lin(out, in_, scale=1.0, bias=0.0, relu=False, on="f"):
+        if relu and SCRATCH[out[0]][2] != "uint16":
+            v = ("ts", (out, in_, bias, 0.0, A.add, A.max) if scale == 1.0 else (out, in_, scale, 0.0, A.mult, A.max))
+        elif scale == 1.0:
+            v = ("cp", (out, in_)) if bias == 0.0 else ("ts", (out, in_, bias, None, A.add, None))
+        else:
+            v = ("ts", (out, in_, scale, bias, A.mult, A.add))
+        func = F.Relu if relu else F.Copy if (scale, bias) == (1.0, 0.0) else F.Identity
+        ways = {"v": v + (cyc(out, [in_], fast(out, in_)),), "a": ("act", (out, in_, func, bias, scale), cyc(out, [in_]))}
+        if on == "f":
+            put("f", "either", ways, [out], [in_, bias, scale], ways["a"][2])
+        else:
+            put(on, ways[on][0], ways[on][1], [out], [in_, bias, scale], ways[on][2])
+
+    def whole(out, in_, tmp, on):
+        if on == "v":
+            ts(out, in_, MAG, A.add, MAG, A.subtract)
+        else:
+            act(tmp, in_, bias=MAG)
+            lin(out, tmp, bias=-MAG)
+
+    def mm(out, lhs, rhs, start, stop):
+        put("p", "mm", (out, lhs, rhs, start, stop), [out], [lhs, rhs], max(64, width(rhs)) * PECY)
+
+    def group(*terms):
+        for i, (o, l, r) in enumerate(terms):
+            mm(o, l, r, i == 0, i == len(terms) - 1)
+
+    def iota(out, pat, base, cm, after=()):
+        put("g", "iota", (out, pat, base, cm), [out], [], 0.13 + 2 * width(out) * CY, after)
+
+    def load(e, name, out, lo=0, ins=(), sem=None):
+        put(e, "load", (out, name, lo, "l_" + (sem or name)), [out], ins, width(out) * SIZE[SCRATCH[out[0]][2]] * DMAB)
+
+    def store(e, name, lo, in_):
+        put(e, "store", (in_, name, lo), [], [in_], width(in_) * SIZE[SCRATCH[in_[0]][2]] * DMAB)
+
+    def send(i):
+        s, d = message(i)
+        k = put("g", "send", (i,), [], [s], 0.3)
+        put("r", "land", (i,), [d], [], HOP, [k])
+        return k
+
+    load("s", "wt", R("WI", 0, 1))
+    load("a", "zt", R("ZB"))
+    load("s", "ch", R("CI"))
+    load("a", "xt", R("TAB", 0, 2048))
+    load("s", "pa", R("PI_"))
+    load("s", "vi", R("QI"))
+    load("s", "de", R("DI", 0, 1))
+    load("s", "pl", R("PLI"), ins=[R("TAB", 0, 2048)])
+    iota(R("PN", 0, 1), [[0, 1]], 0, 1)
+    iota(R("GE"), [[1, 144]], -16, 0)
+    iota(R("B8"), [[1, 8]], 0, 0)
+    iota(R("G"), [[16, 8], [0, 16]], 0, 0)
+    iota(R("KP"), [[0, 8], [1, 16]], 0, 0)
+    for c0, c1 in LANES:
+        iota(R("MK", 16 * c0, 16 * c1), [[0, 16 * (c1 - c0)]], 1, 0)
+    mset(R("ZR"), 0.0)
+    mset(R("C32"), 32.0)
+    mset(R("C128"), 128.0)
+    act(R("CN"), R("ZR"), bias=-LIFT)
+    mset(R("ONE"), 1.0 / 512)
+    ts(R("PN", 1, 2), R("PN", 0, 1), 15, A.bitwise_and)
+    mset(R("OD0"), 0)
+    mset(R("OD1"), 0)
+    cp(R("CF", PF, KF + 1), R("PN"))
+    ts(R("IB"), R("GE", 16, 144), col(PF), A.is_equal)
+    tt(col(G16), col(PF), col(KF), A.subtract)
+    mset(R("CUT"), -1.0)
+    act(col(C16), col(KF), scale=16.0)
+    act(col(C37), col(KF), scale=37.0)
+    act(col(C4), col(KF), scale=4.0)
+    act(col(C4P), col(KF), scale=4.0, bias=512.0)
+    act(R("N2K"), R("IB"), scale=-2048.0)
+    for h in CH:
+        nb = NBS[h]
+        act(R("OFF%d" % h, 0, nb), R("B8", 0, nb), scale=256.0, bias=col(C16))
+        act(R("OFF%d" % h, nb, 2 * nb), R("ZR", 0, nb))
+        act(R("OFF%d" % h, 2 * nb, 3 * nb), R("B8", 0, nb), scale=64.0, bias=col(C4 if h else C4P))
+        act(col(CA + h), col(KF), scale=16.0 * nb, bias=-16.0 * B0[h])
+    for nb in sorted(set(NBS)):
+        q16 = R("OFF%d" % NBS.index(nb), 0, nb)
+        ts(R("PA", 0, nb), q16, 1.0 / (16 * nb), A.mult, 0.5 / nb - 0.5, A.add)
+        act(R("PW", 0, nb), R("PA", 0, nb), scale=1.0 - 16 * nb)
+        tt(R("PERM%d" % NBS.index(nb), 0, nb), R("PW", 0, nb), q16, A.add)
+    ts(R("EBP"), R("GE"), col(G16), A.is_equal, 16384.0, A.mult)
+    for name, scale in (("I16", 1.0), ("NIB", -1.0), ("NI16", -1.0), ("IH16", 0.5)):
+        act(R(name), R("IB"), scale=scale)
+    cp(col(WF), R("WI", 0, 1))
+    ts(col(WG), R("WI", 0, 1), 1.0 / 2048, A.mult)
+    ts(R("GEP"), R("KP", 0, 16), col(KF), A.add, 15.0, A.is_ge)
+    ts(R("WS"), R("G"), col(G16), A.is_equal, col(WG), A.mult)
+    ts(R("W16"), R("G"), col(G16), A.is_equal, col(WF), A.mult)
+    act(R("Z"), R("ZB"), bias=LIFT)
+    group((R("BD0", 0, 1), R("WS"), R("CN", 0, 1)))
+    lin(col(UB), R("BD0", 0, 1), bias=LIFT - 2047.0 / 4096)
+    ts(R("LE"), R("KP", 0, 16), col(KF), A.is_ge)
+    tt(R("WN"), R("W16"), R("N2K"), A.add)
+    rank[0] = LATER
+    for name, scale in (("EBN", -1.0), ("EB2P", 2.0), ("EB2N", -2.0)):
+        act(R(name), R("EBP"), scale=scale)
+    act(R("D0"), R("G"), scale=32641.0, bias=30720.0)
+    ts(R("MKD"), R("KP"), col(KF), A.not_equal, -4194304.0, A.mult)
+    ts(R("RS"), R("KP"), 0.0, A.is_equal, -8388608.0, A.mult)
+    for j in range(16):
+        lin(R("CUT", 128 * j + 112, 128 * j + 128), R("GEP"), R("LE", j, j + 1), -1.0, on="vva"[j % 3])
+    tt(R("D0"), R("D0"), R("KP"), A.add)
+    act(R("WB"), R("W16"))
+    for name, scale in (("IH", 0.5), ("NIH", -0.5), ("I4K", 4096.0), ("N4K", -4096.0)):
+        act(R(name), R("IB"), scale=scale)
+
+    def seq(s, t, h):
+        c0, c1 = LANES[h]
+        if t == 0:
+            return {"x": R("EAR", c0, c1), "y": R("P0", c0, c1), "v": R("EAR", 128 + c0, 128 + c1)}[s]
+        if s == "v":
+            return R("V%d" % t, c0, c1)
+        k = 3 * c0 + "qxy".index(s) * (c1 - c0)
+        return R("S%d_" % t, k, k + c1 - c0)
+
+    def u_of_marks(h):
+        c0, c1 = LANES[h]
+        n = c1 - c0
+        u1, u2 = R("BU%d" % h, 128, 128 + n), R("BU%d" % h, 0, n)
+        group((u1, R("WS"), R("Z", c0, c1)))
+        lin(R("FU", c0, c1), u1, bias=col(UB))
+        group((u2, R("IB"), R("C32", 0, n)), (u2, R("WN"), R("CN", 0, n)), (u2, R("W16"), R("Z", c0, c1)),
+              (u2, R("N2K"), R("FU", c0, c1)))
+
+    def lists(s, t, h):
+        c0, c1 = LANES[h]
+        stage("l" + s, t, h)
+        tt(R("H" + s, c0, c1), R("BU%d" % h, 0, c1 - c0), seq(s, t, h), A.mult)
+        ts(R("G" + s, c0, c1), R("H" + s, c0, c1), 5, A.logical_shift_right, 2047, A.bitwise_and)
+        lin(R("I" + s, c0, c1), (R("G" + s, c0, c1), R("PERM%d" % NBS.index(NBS[h]), 0, NBS[h])), bias=col(C37))
+
+    def select(h, ct, keep, take, out, name="C"):
+        n, m = width(ct), width(out)
+        parts = range(0, m, n)
+        first = [] if m == n else [(R("BG1", 0, m), R("ZR"), R("CUT", 0, m))]
+        group(*(first + [(R("BG1", k, k + n), R("I16"), keep[k // n]) for k in parts]
+                + [(R("BG1", k, k + n), R("N4K"), ct) for k in parts]))
+        group(*([(R("BG2", 0, m), R("I16"), take)] + [(R("BG2", k, k + n), R("I4K"), ct) for k in parts]))
+        kept = R("KEEP", 2 * LANES[h][0], 2 * LANES[h][0] + m)
+        label.append("K" + name)
+        lin(kept, R("BG1", 0, m), bias=-4096.0, relu=True)
+        label.append(name)
+        tt(out, R("BG2", 0, m), kept, A.max)
+
+    bank = [0]
+
+    def gathers(t, h, which):
+        nb = NBS[h]
+        c0, c1 = LANES[h]
+        w = 16 * nb
+        sums = R("BD%d" % h, 0, w)
+
+        def dsum(a0, a1, buf, eb):
+            for a in range(a0, a1):
+                lo = 16 * c0 + w * a
+                lhs, rhs = R(eb, 16 - a, 144 - a), R(buf, lo, lo + w)
+                put("p", "sum", (sums, lhs, rhs, (t, h)), [sums], [lhs, rhs], max(64, w) * PECY)
+
+        for s, way, a0, a1 in PLAN[h]:
+            lo, hi = 16 * c0 + w * a0, 16 * c0 + w * a1
+            lst = (R("TAB", 0, 2048 + EXT), R("I" + s, lo // 16, hi // 16))
+            xs = R("X", lo, hi)
+            stage(s, t, h)
+            if s not in which:
+                continue
+            if s == "x":
+                lin(xs, lst, on=way)
+                continue
+            dd, aa = ("DY", "AY") if s == "y" else ("DV", "AV")
+            one, two, neg = ("EBN", "EB2N", "EBP") if s == "y" else ("EBP", "EB2P", "EBN")
+            if way == "S":
+                act(R(dd, lo, hi), lst, F.Copy)
+                df = R("BF%d" % (bank[0] % 2), 0, hi - lo)
+                bank[0] += 1
+                group((df, R("NIB"), xs), (df, R("IB"), R(dd, lo, hi)))
+                act(R(aa, lo, hi), df, F.Abs)
+                dsum(a0, a1, aa, one)
+                continue
+            tt(R(dd, lo, hi), lst, xs, A.subtract)
+            if way == "V":
+                dsum(a0, a1, dd, neg)
+                ts(R(aa, lo, hi), R(dd, lo, hi), 0.0, A.max)
+                dsum(a0, a1, aa, two)
+            else:
+                act(R(aa, lo, hi), R(dd, lo, hi), F.Abs)
+                dsum(a0, a1, aa, one)
+
+    def cut(t, h):
+        last = t == VIS - 1
+        nb, b0 = NBS[h], B0[h]
+        c0, c1 = LANES[h]
+        n, x0, x1 = c1 - c0, 16 * c0, 16 * c1
+        ln = lambda name: R(name, c0, c1)
+        bl = lambda name: R(name, b0, b0 + nb)
+        own = lambda name, k0, k1: R("%s%d" % (name, h), k0 * nb, k1 * nb)
+        stage("cut", t, h)
+        ts(ln("SG"), R("BD%d" % h, 0, n), -16384.0, A.max, 16384.0, A.min)
+        scan(ln("S1"), ln("D0"), ln("SG"), 0.0, A.max, A.subtract)
+        scan(ln("S2"), ln("C128"), ln("S1"), 0.0, A.add, A.max)
+        end = R("S2", c0 + 15, c1, 16)
+        tt(own("KK", 0, 1), end, bl("BT" if t else "BOFF"), A.subtract)
+        lin(own("KK", 1, 2), end, -1.0 / 128, -129.0 / 256)
+        ts(own("AA", 0, 2), own("KK", 0, 2), 127, A.bitwise_and)
+        lin(own("OO", 0, 2), own("AA", 0, 2), bias=col(CA + h))
+        oi, oe = own("OO", 0, 1), own("OO", 1, 2)
+        stage("rec", t, h)
+        ts(bl("CD"), own("KK", 0, 1), 0x8078F, A.bitwise_and)
+        oc = own("OD" if t == 0 else "OC", 0, 1)
+        label.append("OC")
+        lin(oc, bl("CD"), -1.0, 2047.0, relu=True)
+        sent = send(1 + h) if t == 0 else None
+        x, y, q = seq("x", t, h), seq("y", t, h), seq("q", t + 1, h)
+        short = QUICK[h] and 0 < t < VIS - 1
+        if short:
+            group((R("BG1", 0, n), R("I16"), x), (R("BG1", 0, n), R("NI16"), seq("v", t, h)))
+            lin(ln("DQ"), R("BG1", 0, n))
+            tt(ln("TQ"), (R("CUT"), oc), ln("DQ"), A.mult)
+            label.append("Q")
+            tt(q, ln("TQ"), x, A.add)
+            sent = send(1 + len(NBS) * t + h)
+            stage("child", t, h)
+        lin(ln("CT"), (R("CUT"), oc))
+        if t == 0 or short:
+            select(h, ln("CT"), [x], y, seq("x", t + 1, h))
+        else:
+            select(h, ln("CT"), [seq("v", t, h), x], (x[0], x[1], y[2]), (q[0], q[1], q[2] + n))
+            if last:
+                store("s", "yq", c0, q)
+                store("s", "yc", c0, seq("x", t + 1, h))
+            else:
+                sent = send(1 + len(NBS) * t + h)
+        stage("val", t, h)
+        nn, cd = bl("NN"), bl("CD")
+        put("f", "either", {"v": ("ts", (nn, cd, 524288.0, 512.0, A.is_ge, A.mult), cyc(nn, [cd])),
+                            "a": ("act", (nn, cd, F.Relu, -2.0, 513.3 / 524288), cyc(nn, [cd]))}, [nn], [cd], cyc(nn, [cd]))
+        lin(ln("GX"), (R("X", x0, x1), oi))
+        lin(ln("GD"), (R("DV", x0, x1), oi))
+        val = R("BF0" if h == CH[-1] else "BD0", 0, n)
+        plain = [(16 * b + a0, 16 * b + a1) for s, way, a0, a1 in PLAN[h] if s + way == "vS" for b in range(nb)]
+        group(*([(val, R("IB"), ln("GX"))]
+                + [(R(val[0], lo, hi), R("NIH"), R("GX", c0 + lo, c0 + hi)) for lo, hi in plain]
+                + [(val, R("IH"), ln("GD"))]))
+        lin(ln("VAL"), val, bias=-0.25)
+        stage("max", t, h)
+        cp((R("MK", x0, x1), oi), R("ZR", 0, n))
+        step = (x1 - x0) // PIECES[h]
+        for k in range(x0, x1, step):
+            scan(R("SC", k, k + step), R("MK", k, k + step), R("X", k, k + step), 0.0, A.mult, A.max)
+        lin(ln("MM"), (R("SC", x0, x1), oe))
+        um = R("BD%d" % h, 0, n)
+        group((um, R("IB"), ln("MKD")), (um, R("WB"), ln("MM")))
+        scan(ln("SU"), ln("RS"), um, -8388608.0, A.add, A.max)
+        stage("place", t, h)
+        for k, mask in enumerate((15, 511, 3)):
+            ts(own("AT", k, k + 1), R("SU", c0 + 15, c1, 16), mask, A.bitwise_and)
+        off = "BF1" if h == CH[-1] else "BD0"
+        group((R(off, 0, 3 * nb), R("I16"), own("OFF", 0, 3)),
+              (R(off, 2 * nb, 3 * nb), R("IB" if h else "NIB"), bl("NN")))
+        tt(own("OL", 0, 3), R(off, 0, 3 * nb), own("AT", 0, 3), A.add)
+        label.append("P")
+        lin(seq("y", t + 1, h), (R("POOL", 512, 1024), own("OL", 1, 2)))
+        stage("mark", t, h)
+        zp = R("BU%d" % h, 256, 256 + n)
+        group((zp, R("IH16"), ln("Z")), (zp, R("IH"), ln("MM")))
+        lin(ln("Z"), zp, bias=LIFT / 2 - 0.25)
+        if last:
+            store("s", "yp", c0, seq("y", t + 1, h))
+            lin(ln("ZB"), ln("Z"), bias=-LIFT)
+            store("s", "yz", c0, ln("ZB"))
+        else:
+            u_of_marks(h)
+        return sent
+
+    def writes(t, h):
+        last = t == VIS - 1
+        nb = NBS[h]
+        c0, c1 = LANES[h]
+        stage("tab", t, h)
+        cp((R("TAB", 16 * c0, 16 * c1), R("OL%d" % h, 0, nb)), R("VAL", c0, c1))
+        if last:
+            store("s", "yx", 16 * c0, R("TAB", 16 * c0, 16 * c1))
+        elif h == 0:
+            cp((R("TAB", 2048, 2048 + 768), R("OL0", 0, 3)), R("VAL", 0, 48))
+
+    def pool_writes(t, h):
+        nb = NBS[h]
+        c0, c1 = LANES[h]
+        stage("pool", t, h)
+        pool = "POOL2" if t == VIS - 1 else "POOL"
+        win = R(pool, 512 + 4 * c0, 1536) if h else R(pool, 0, 512 + 4 * c1)
+        label.append("POOL")
+        cp((win, R("OL%d" % h, 2 * nb, 3 * nb)), seq("x", t + 1, h))
+        if t == VIS - 1:
+            store("a", "yl", 4 * c0, R(pool, 512 + 4 * c0, 512 + 4 * c1))
+        elif t == VIS - 2 and h == CH[-1]:
+            put("s", "copy", (R("POOL2", 512, 1024), R("POOL", 512, 1024), "l_x2"), [R("POOL2", 512, 1024)],
+                [R("POOL", 512, 1024)], 2048 * DMAB)
+
+    stage("rec", 0)
+    label.extend(["EXT", "PI", "QI", "CI", "BOFF", "TH"])
+    lin(col(CTHR), R("DI", 0, 1), 16384.0, 16384.0)
+    lin(R("BOFF"), R("B8"), 524288.0, col(CTHR))
+    stage("lx", 0)
+    lin(R("EAR", 0, 128), R("CI"))
+    lin(R("EAR", 128, 256), R("QI"))
+    lin(R("P0"), R("PI_"))
+    lin(R("TAB", 2048, 2048 + EXT), R("TAB", 0, EXT), on="v")
+    send(0)
+    for h in CH:
+        stage("lx", 0, h)
+        label.append("U")
+        u_of_marks(h)
+        lists("x", 0, h)
+        lists("y", 0, h)
+    stage("rec", 0)
+    label.append("PL")
+    lin(R("POOL", 512, 1024), R("PLI"))
+    for t in range(VIS):
+        last = t == VIS - 1
+        for h in CH:
+            gathers(t, h, "xy")
+        for h in CH:
+            if t == 1:
+                c0, c1 = LANES[h]
+                stage("lv", t, h)
+                lin(R("CTV", c0, c1), (R("CUT"), R("CL%d" % h, 0, NBS[h])))
+                select(h, R("CTV", c0, c1), [R("EL", 128 + c0, 128 + c1)], R("EL", c0, c1), seq("v", 1, h), "V")
+            lists("v", t, h)
+            gathers(t, h, "v")
+        for h in CH:
+            sent = cut(t, h)
+            if not last:
+                lists("x", t + 1, h)
+                lists("y", t + 1, h)
+        for h in CH:
+            writes(t, h)
+        for h in CH:
+            pool_writes(t, h)
+        if not last:
+            stage("count", t)
+            for c0, c1 in LANES:
+                iota(R("MK", 16 * c0, 16 * c1), [[0, 16 * (c1 - c0)]], 1, 0, [sent])
+            cnt = R("BG1", 0, 1)
+            group(*[(cnt, R("ONE"), R("NN", b, b + 1)) for b in range(8)])
+            lin(col(CF1), cnt, 0.4999, MAG)
+            lin(col(CF2), col(CF1), -32768.0, 32768.0 * MAG)
+            lin(col(THR), cnt, 16384.0, col(CF2))
+            lin(R("BT"), R("BOFF"), bias=col(THR))
+    return calls
+
+
+def needs(calls):
+    acc, dep = {}, []
+    for i, (e, kind, args, rd, wr, cost, after, rank, tag) in enumerate(calls):
+        d = {k: calls[k][0] != e for k in after}
+        for regs, w in ((rd, False), (wr, True)):
+            for n, lo, hi in regs:
+                bank = SCRATCH[n][0] == "psum"
+                for l2, h2, w2, j in acc.get(n, []):
+                    e2 = calls[j][0]
+                    if bank and e == e2 == "p":
+                        if not (kind == "sum" == calls[j][1] and args[3] == calls[j][2][3]):
+                            d.setdefault(j, False)
+                    elif (bank and (e2 != e or e == "f" or w or w2)) or (l2 < hi and lo < h2 and (w or w2)):
+                        d[j] = True
+        for regs, w in ((rd, False), (wr, True)):
+            for n, lo, hi in regs:
+                old = acc.get(n, [])
+                if w and SCRATCH[n][0] == "psum":
+                    old = old if kind == "sum" else []
+                elif w:
+                    old = [x for x in old if not (lo <= x[0] and x[1] <= hi)]
+                acc[n] = old + [(lo, hi, w, i)]
+        dep.append(d)
+    return dep
+
+
+def order(calls, dep):
+    n = len(calls)
+    users = [[] for _ in range(n)]
+    for i in range(n):
+        for j in dep[i]:
+            users[j].append(i)
+    rank = [c[7] for c in calls]
+    for i in range(n - 1, -1, -1):
+        rank[i] = min([rank[i]] + [rank[u] for u in users[i] if INHERIT])
+    left, since = [len(d) for d in dep], [{q: 0.0 for q in ("va" if c[0] == "f" else c[0])} for c in calls]
+    ready = [i for i in range(n) if not left[i]]
+    free = {e: 0.0 for e in "vapgsrd"}
+    out, span = [], 0.0
+    while ready:
+        at, on = {}, {}
+        for i in ready:
+            on[i] = calls[i][0]
+            if on[i] == "f":
+                on[i] = "v" if max(since[i]["v"], free["v"]) + SLACK < max(since[i]["a"], free["a"]) else "a"
+                if calls[i][8] and ON.get(calls[i][8][1], "f") != "f":
+                    on[i] = ON[calls[i][8][1]]
+            at[i] = max(since[i][on[i]], free[on[i]])
+        i = min(ready, key=lambda i: (at[i], rank[i], i))
+        e = on[i]
+        if calls[i][5] > LONG:
+            u = min((k for k in ready if on[k] == e and at[k] <= at[i] + SOON), key=lambda k: (rank[k], at[k], k))
+            fits = [k for k in ready if on[k] == e and at[k] + calls[k][5] <= at[u] + FIT]
+            i = min(fits, key=lambda k: (at[k], rank[k], k)) if fits and at[u] > at[i] else u
+        if calls[i][0] == "f":
+            kind, args, cost = calls[i][2][e]
+            calls[i] = (e, kind, args) + calls[i][3:5] + (cost,) + calls[i][6:]
+        ready.remove(i)
+        end = at[i] + calls[i][5]
+        if calls[i][1] in ("load", "store", "copy"):
+            free[e] = at[i] + 0.05
+            end = free["d"] = max(free["d"], at[i] + DMA0) + calls[i][5] + ROWS
+        elif e != "r":
+            free[e] = end
+        out.append(i)
+        span = max(span, end)
+        for u in users[i]:
+            for q in since[u]:
+                since[u][q] = max(since[u][q], end + ((NEAR if q == e else WAKE) if dep[u][i] else 0.0))
+            left[u] -= 1
+            if not left[u]:
+                ready.append(u)
+    return out, span
+
+
+def places(text):
+    out = {}
+    for k, word in enumerate(text.split()):
+        name, _, e = word.lstrip("<>").partition("@")
+        out[name] = (k + 1000 * (word.count(">") - word.count("<")), e)
+    return out
+
+
+def listed(calls, dep, usual, final, first):
+    n = len(calls)
+    users = [[] for _ in range(n)]
+    key = [None] * n
+    for i, c in enumerate(calls):
+        for j in dep[i]:
+            users[j].append(i)
+        place, e = {0: first, VIS - 1: final}.get(c[8][0], usual).get(c[8][1], (None, "")) if c[8] else (None, "")
+        if place is not None:
+            key[i] = 1000 * c[8][0] + place
+        elif c[1] == "load" or c[0] in "vaf" and not c[8]:
+            key[i] = c[7] + 0.001 * i
+        if c[0] == "f":
+            kind, args, cost = c[2][e or "a"]
+            calls[i] = (e or "a", kind, args) + c[3:5] + (cost,) + c[6:]
+    for i in range(n - 1, -1, -1):
+        if key[i] is None:
+            key[i] = min([key[u] for u in users[i]] or [1000 * VIS]) - 0.001
+    for i in range(n):
+        key[i] = max([key[i]] + [key[j] for j in dep[i]])
+    start, end = [0.0] * n, [0.0] * n
+    free = {e: 0.0 for e in "vad"}
+    for i in sorted(range(n), key=lambda i: (key[i], i)):
+        e, kind = calls[i][:2]
+        t = max([free.get(e, 0.0)] + [end[j] + ((NEAR if calls[j][0] == e else WAKE) if w else 0.0)
+                                      for j, w in dep[i].items()])
+        start[i], end[i] = t, t + calls[i][5]
+        if kind in ("load", "store", "copy"):
+            end[i] = free["d"] = max(free["d"], t + DMA0) + calls[i][5]
+        elif e in free:
+            free[e] = end[i]
+    return sorted(range(n), key=lambda i: (start[i], key[i], i))
+
+
+PLANNED = []
+
+
+def planned():
+    if not PLANNED:
+        calls = program()
+        dep = needs(calls)
+        seq = order(calls, dep)[0]
+        sums = {}
+        for i in seq:
+            if calls[i][1] == "sum":
+                sums.setdefault(calls[i][2][3], []).append(i)
+        for terms in sums.values():
+            for i in terms:
+                calls[i] = ("p", "mm", calls[i][2][:3] + (i == terms[0], i == terms[-1])) + calls[i][3:]
+        PLANNED.extend([calls, dep, seq])
+    return PLANNED
+
+
 def relay_program(g, core, T, topo, src, dst):
     n_in = len(topo.engines(src, core))
     n_out = len(topo.engines(core, dst))
     rid, pid = topo.addr(dst, core)
-    for i in range(VIS):
-        n, a, b = message(T, i)[1]
-        g.wait_ge(T.sem["m%d" % i], n_in)
-        g.remote_dma(T[n][:, a:b], T[n][:, a:b], T.sem["m%d" % i], T.sem.ls, pid, rid, topo.mask(core, dst))
-    g.wait_ge(T.sem.ls, n_out * VIS)
+    calls, dep, seq = planned()
+    for k in seq:
+        if calls[k][1] == "send":
+            i = calls[k][2][0]
+            n, a, b = message(i)[1]
+            g.wait_ge(T.sem["m%d" % i], n_in)
+            g.remote_dma(T[n][:, a:b], T[n][:, a:b], T.sem["m%d" % i], T.sem.ls, pid, rid, topo.mask(core, dst))
+    g.wait_ge(T.sem.ls, n_out * NMSG)
 
 
 def rank_program(g, core, T, topo):
@@ -110,488 +693,73 @@ def rank_program(g, core, T, topo):
     n_out = len(topo.engines(core, nxt))
     n_in = len(topo.engines(prv, core))
     rid, pid = topo.addr(nxt, core)
-
     Q = {"v": g.vector, "a": g.scalar, "p": g.tensor, "g": g, "s": g.sync}
-    cnt = {}
+
+    def ap(x):
+        if not isinstance(x, tuple):
+            return x
+        if isinstance(x[0], tuple):
+            return ap(x[0]).indirect(ap(x[1]))
+        return T[x[0]][:, x[1]:x[2]:x[3]] if len(x) == 4 else T[x[0]][:, x[1]:x[2]]
+
+    def hbm(name, lo, r):
+        return T[name][:] if width(r) == T[name].shape[1] else T[name][:, lo:lo + width(r)]
+
+    def issue(e, kind, a):
+        if kind == "land":
+            return "m%d" % a[0], n_in
+        if kind == "send":
+            s, d = message(a[0])
+            g.remote_dma(ap(d), ap(s), T.sem["m%d" % a[0]], T.sem.ls, pid, rid, topo.mask(core, nxt))
+            return "ls", n_out
+        if kind == "load":
+            Q[e].dma_start(ap(a[0]), hbm(a[1], a[2], a[0])).then_inc(T.sem[a[3]], 16)
+            return a[3], 16
+        if kind == "copy":
+            Q[e].dma_start(ap(a[0]), ap(a[1])).then_inc(T.sem[a[2]], 16)
+            return a[2], 16
+        if kind == "store":
+            Q[e].dma_start(hbm(a[1], a[2], a[0]), ap(a[0])).then_inc(T.sem.out, 16)
+            return "out", 16
+        x = [ap(v) for v in a]
+        if kind == "cp":
+            ins = g.vector.tensor_copy(*x)
+        elif kind == "tt":
+            ins = g.vector.tensor_tensor(*x)
+        elif kind == "ts":
+            ins = g.vector.tensor_scalar(*(x if x[5] is not None else x[:5]))
+        elif kind == "scan":
+            ins = g.vector.tensor_tensor_scan(*x)
+        elif kind == "mset":
+            ins = g.vector.memset(*x)
+        elif kind == "act":
+            ins = g.scalar.activation(x[0], x[1], x[2], bias=x[3], scale=x[4])
+        elif kind == "mm":
+            ins = g.tensor.matmul(*x)
+        elif SCRATCH[a[0][0]][2] == "int32":
+            ins = g.iota(*x)
+        else:
+            ins = g.iota(*x, allow_small_or_imprecise_dtypes=True)
+        ins.then_inc(T.sem["s" + e], 1)
+        return "s" + e, 1
+
+    calls, dep, seq = planned()
+    cnt, mark = {}, {}
     seen = {e: {} for e in Q}
-    acc = {}
-
-    def touch(e, regs, wr, need):
-        for (n, lo, hi) in regs:
-            ps = SCRATCH[n][0] == "psum"
-            for (l2, h2, w2, e2, s2, c2) in acc.get(n, []):
-                if ps:
-                    hit = (e2 != e) or (e != "p" and (wr or w2))
-                else:
-                    hit = l2 < hi and lo < h2 and (wr or w2)
-                if hit and need.get(s2, 0) < c2:
-                    need[s2] = c2
-
-    def note(e, regs, wr, s, c):
-        for (n, lo, hi) in regs:
-            old = acc.get(n, [])
-            if wr:
-                old = [x for x in old if not (lo <= x[0] and x[1] <= hi)]
-            else:
-                old = [x for x in old if not (x[3] == e and x[4] == s and not x[2] and lo <= x[0] and x[1] <= hi)]
-            old.append((lo, hi, wr, e, s, c))
-            acc[n] = old
-
-    def op(e, fn, rd, wr, sem=None, inc=1, attach=True):
-        need = {}
-        touch(e, rd, False, need)
-        touch(e, wr, True, need)
-        for s2 in sorted(need):
-            if seen[e].get(s2, 0) < need[s2]:
-                Q[e].wait_ge(T.sem[s2], need[s2])
-                seen[e][s2] = need[s2]
-        s = sem or ("s" + e)
-        ins = fn()
-        if attach:
-            ins.then_inc(T.sem[s], inc)
+    for i in seq:
+        e, kind, args = calls[i][:3]
+        if e != "r":
+            need = {}
+            for j, wait in dep[i].items():
+                if wait:
+                    s, c = mark[j]
+                    need[s] = max(need.get(s, 0), c)
+            for s in sorted(need):
+                if seen[e].get(s, 0) < need[s]:
+                    Q[e].wait_ge(T.sem[s], need[s])
+                    seen[e][s] = need[s]
+        s, inc = issue(e, kind, args)
         cnt[s] = cnt.get(s, 0) + inc
-        note(e, rd, False, s, cnt[s])
-        note(e, wr, True, s, cnt[s])
-
-    def ap(r):
-        if len(r) == 4:
-            return T[r[0]][:, r[1]:r[2]:r[3]]
-        return T[r[0]][:, r[1]:r[2]]
-
-    def R(n, lo=0, hi=None, st=None):
-        if hi is None:
-            hi = SCRATCH[n][1][1]
-        return (n, lo, hi) if st is None else (n, lo, hi, st)
-
-    def col(c):
-        return ("CF", c, c + 1)
-
-    def r3(x):
-        return x[:3]
-
-    def src(x):
-        if isinstance(x[0], tuple):
-            return ap(x[0]).indirect(ap(x[1])), [r3(x[0]), r3(x[1])]
-        return ap(x), [r3(x)]
-
-    def dstp(x):
-        if isinstance(x[0], tuple):
-            return ap(x[0]).indirect(ap(x[1])), [r3(x[0])], [r3(x[1])]
-        return ap(x), [r3(x)], []
-
-    def scal(s):
-        if isinstance(s, tuple):
-            return ap(s), [r3(s)]
-        return s, []
-
-    def cp(out, in_):
-        o, w, r0 = dstp(out)
-        i, r1 = src(in_)
-        op("v", lambda: g.vector.tensor_copy(o, i), r0 + r1, w)
-
-    def tt(out, in0, in1, alu):
-        i, r1 = src(in0)
-        op("v", lambda: g.vector.tensor_tensor(ap(out), i, ap(in1), alu), r1 + [r3(in1)], [r3(out)])
-
-    def ts(out, in0, s1, o0, s2=None, o1=None):
-        a1, r1 = scal(s1)
-        a2, r2 = scal(s2)
-        i, r0 = src(in0)
-        if o1 is None:
-            fn = lambda: g.vector.tensor_scalar(ap(out), i, a1, None, o0)
-        else:
-            fn = lambda: g.vector.tensor_scalar(ap(out), i, a1, a2, o0, o1)
-        op("v", fn, r0 + r1 + r2, [r3(out)])
-
-    def scan(out, d0, d1, init, o0, o1):
-        op("v", lambda: g.vector.tensor_tensor_scan(ap(out), ap(d0), ap(d1), init, o0, o1), [r3(d0), r3(d1)], [r3(out)])
-
-    def mset(out, v):
-        op("v", lambda: g.vector.memset(ap(out), v), [], [r3(out)])
-
-    def act(out, in_, func=F.Identity, bias=0.0, scale=1.0, accum=None):
-        i, r1 = src(in_)
-        b, r2 = scal(bias)
-        s, r4 = scal(scale)
-        if accum is None:
-            op("a", lambda: g.scalar.activation(ap(out), i, func, bias=b, scale=s), r1 + r2 + r4, [r3(out)])
-        else:
-            op("a", lambda: g.scalar.activation(ap(out), i, func, bias=b, scale=s, accum_out=ap(accum)),
-               r1 + r2 + r4, [r3(out), r3(accum)])
-
-    def mm(out, lhs, rhs, start, stop):
-        op("p", lambda: g.tensor.matmul(ap(out), ap(lhs), ap(rhs), start, stop), [r3(lhs), r3(rhs)], [r3(out)])
-
-    def iota(out, pat, base, cm, flag=True):
-        if flag:
-            fn = lambda: g.iota(ap(out), pat, base, cm, allow_small_or_imprecise_dtypes=True)
-        else:
-            fn = lambda: g.iota(ap(out), pat, base, cm)
-        op("g", fn, [], [r3(out)])
-
-    def load(e, name, out):
-        op(e, lambda: Q[e].dma_start(ap(out), T[name][:]), [], [out], "l_" + name, 16)
-
-    def store(e, name, in_):
-        op(e, lambda: Q[e].dma_start(T[name][:], ap(in_)), [in_], [], "o_" + name, 16)
-
-    def send(i):
-        s, d = message(T, i)
-        op("g", lambda: g.remote_dma(ap(d), ap(s), T.sem["m%d" % i], T.sem.ls, pid, rid, topo.mask(core, nxt)),
-           [s], [], "ls", n_out, False)
-
-    for i in range(VIS):
-        cnt["m%d" % i] = n_in
-        note("r", [message(T, i)[1]], True, "m%d" % i, n_in)
-
-    def P_(t):
-        return R("S3%d" % t, 0, 128)
-
-    def C_(t):
-        return R("S3%d" % t, 128, 256)
-
-    def V_(t):
-        return R("S3%d" % t, 256, 384)
-
-    U1, U2 = R("B1", 0, 128), R("B2", 0, 128)
-
-    load("s", "wt", R("WI", 0, 1))
-    load("s", "zt", R("ZB"))
-    load("s", "ch", R("CI"))
-    load("a", "xt", R("TAB", 0, 2048))
-    ext = R("TAB", 2048, 2048 + EXT)
-    op("a", lambda: g.scalar.dma_start(ap(ext), T.xt[:, 0:EXT]), [], [ext], "l_x2", 16)
-    load("s", "pa", R("PI_"))
-    load("s", "vi", R("QI"))
-    load("s", "de", R("DI", 0, 1))
-    op("s", lambda: g.sync.dma_start(ap(R("PLI")), T.pl[:]), [R("TAB")], [R("PLI")], "l_pl", 16)
-    iota(R("PN"), [[0, 1]], 0, 1, False)
-    iota(R("G"), [[16, 8], [0, 16]], 0, 0)
-    iota(R("B8"), [[1, 8]], 0, 0)
-    iota(R("GE"), [[1, 144]], -16, 0)
-    iota(R("KP"), [[0, 8], [1, 16]], 0, 0)
-    iota(R("P8"), [[64, 2], [4, 4]], 0, 0)
-    iota(R("MK"), [[0, 2048]], 1, 0)
-    mset(R("CUT"), 0.0)
-    ts(R("KN"), R("PN"), 15, A.bitwise_and)
-    cp(col(PF), R("PN"))
-    cp(col(KF), R("KN"))
-    ts(R("R7"), R("PN"), 3, A.bitwise_and)
-    tt(col(G16), col(PF), col(KF), A.subtract)
-    ts(R("GEP", 0, 16), R("KP", 0, 16), col(KF), A.is_le)
-    ts(R("LE"), R("KP", 0, 16), col(KF), A.add, 15.0, A.is_le)
-    ts(R("C2A"), R("G"), 0.0, A.mult, -1023.5 / 16, A.add)
-    ts(R("C2B"), R("G"), 0.0, A.mult, 2.0, A.add)
-    ts(R("J16"), R("G"), col(G16), A.is_equal)
-    ts(R("I32"), R("GE", 16, 144), col(PF), A.is_equal)
-    ts(R("R8"), R("PN"), 2, A.logical_shift_right, 3, A.bitwise_and)
-    ts(col(T7), R("R7"), 16.0, A.mult)
-    ts(R("EBP"), R("GE"), col(G16), A.is_equal, 16384.0, A.mult)
-    ts(R("NE"), R("KP"), col(KF), A.not_equal)
-    ts(col(WH), R("WI", 0, 1), 0.5, A.mult)
-    ts(R("Z2"), R("ZB"), 2.0, A.mult)
-    ts(R("WM"), R("G"), col(G16), A.is_equal, col(WH), A.mult)
-    tt(col(PB), col(T7), R("R8"), A.add)
-    cp(C_(0), R("CI"))
-    ts(col(C37), col(KF), 37.0, A.mult)
-    ts(R("PERM"), R("P8"), col(PB), A.add)
-
-    act(col(CA), col(KF), scale=64.0)
-    act(col(CE), col(KF), scale=64.0, bias=127.0)
-    act(col(CE1), col(KF), scale=64.0, bias=63.0)
-    act(col(C16), col(KF), scale=16.0)
-    act(R("BOFF"), R("B8"), scale=524288.0)
-    act(R("D0"), R("G"), scale=32641.0, bias=30720.0)
-    act(R("BT"), R("B8"), scale=256.0, bias=col(C16))
-    act(R("BP"), R("BT"), scale=0.25)
-    act(R("BT"), R("BT"), bias=7.5)
-    for e1 in range(16):
-        act(R("CUT", 128 * e1, 128 * e1 + 16), R("GEP", 0, 16), F.Copy, scale=R("LE", e1, e1 + 1))
-    act(R("NI32"), R("I32"), scale=-1.0)
-    act(R("EBN"), R("EBP"), scale=-1.0)
-    for tk in PLAN:
-        if tk[:2] == ("r", "v"):
-            act(R("EB2P"), R("EBP"), scale=2.0)
-            break
-    for tk in PLAN:
-        if tk[:2] == ("r", "y"):
-            act(R("EB2N"), R("EBP"), scale=-2.0)
-            break
-    act(R("IB"), R("I32"))
-    act(R("NIB"), R("I32"), scale=-1.0)
-    act(R("I2B"), R("I32"), scale=2.0)
-    act(R("I4K"), R("I32"), scale=4096.0)
-    act(R("IN2K"), R("I32"), scale=-2048.0)
-    act(R("ZZ"), R("ZB"), bias=2047.5)
-    act(R("MKD"), R("NE"), scale=-4194304.0, bias=-7.5)
-
-    def u_pre():
-        mm(U1, R("J16"), R("C2A"), True, False)
-        mm(U1, R("WM"), R("C1"), False, False)
-        mm(U2, R("J16"), R("C2B"), True, False)
-        mm(U2, R("WM"), R("C1"), False, False)
-
-    def u_main():
-        mm(U1, R("WM"), R("Z2"), False, True)
-        mm(U2, R("WM"), R("Z2"), False, True)
-
-    def idx_steps(n, s):
-        return [lambda: tt(R("H" + s), U2, n, A.mult),
-                lambda: ts(R("G" + s), R("H" + s), 5, A.logical_shift_right, 2047, A.bitwise_and),
-                lambda: ts(R("I" + s.upper()), (R("G" + s), R("PERM")), col(C37), A.add)]
-
-    def weave(*chains):
-        k = max(len(c) for c in chains)
-        for i in range(k):
-            for c in chains:
-                if i < len(c):
-                    c[i]()
-
-    mm(U1, R("J16"), R("C2A"), True, False)
-    mm(U2, R("J16"), R("C2B"), True, False)
-    u_main()
-    ts(R("FU"), U1, MAG11, A.add, MAG11, A.subtract)
-    cp(col(WF), R("WI", 0, 1))
-    tt(U2, U2, R("FU"), A.subtract)
-    mset(R("ZR"), 0.0)
-    weave(idx_steps(C_(0), "x"),
-          [lambda: cp(P_(0), R("PI_")),
-           lambda: cp(R("EAR", 128, 256), R("QI")),
-           lambda: mset(R("ONESB"), 1.0)])
-    late = [lambda: ts(R("I16"), R("GE", 16, 144), col(PF), A.is_equal),
-            lambda: ts(R("WB"), R("G"), col(G16), A.is_equal, col(WF), A.mult),
-            lambda: ts(R("C1"), R("G"), 0.0, A.mult, -2048.0, A.add),
-            lambda: mset(R("C128"), 128.0),
-            lambda: ts(R("RS"), R("KP"), 0.0, A.is_equal, -8388608.0, A.mult)]
-
-    dbank = ("B7", "B0")
-
-    def dmm(j, buf, eb, start, stop):
-        for s_ in range(2):
-            a = 2 * (j % 8) + s_
-            mm(R(dbank[j // 8], 0, 64), R(eb, 16 - a, 144 - a), R(buf, 128 * j + 64 * s_, 128 * j + 64 * s_ + 64),
-               start and s_ == 0, stop and s_ == 1)
-
-    n_dmm = [sum(1 for tk in PLAN if tk[0] in ("l", "r", "b", "c") for j in range(tk[2], tk[3]) if j // 8 == h)
-             for h in range(2)]
-    plain_v = [a for tk in PLAN if tk[0] == "g" and tk[1] == "v" for a in range(tk[2], tk[3])]
-
-    for t in range(VIS):
-        last = t == VIS - 1
-        qsel = t > 0
-        vq = V_(t) if t > 0 else R("EAR", 128, 256)
-        ix = {"y": idx_steps(P_(t), "y"), "v": idx_steps(vq, "v")}
-        if t == 0:
-            fill = [lambda: tt(R("EAR", 0, 128), C_(0), R("EAR", 128, 256), A.subtract),
-                    lambda: send(0),
-                    lambda: ts(col(CTHR), R("DI", 0, 1), 16384.0, A.mult, 16384.0, A.add),
-                    lambda: tt(R("D0"), R("D0"), R("KP"), A.add),
-                    lambda: cp(R("POOL", 0, 512), R("PLI"))]
-        else:
-            fill = [lambda: ts(R("A3"), R("KI"), 3, A.bitwise_and),
-                    lambda: tt(R("NB"), R("NN"), R("BP"), A.add),
-                    lambda: tt(R("AP"), R("A3"), R("NB"), A.add),
-                    lambda: cp(R("OP"), R("AP")),
-                    lambda: cp((R("POOL"), R("OP")), C_(t))]
-        done = [0, 0]
-
-        def dsum(j, buf, eb):
-            h = j // 8
-            dmm(j, buf, eb, done[h] == 0, done[h] == n_dmm[h] - 1)
-            done[h] += 1
-
-        def half(h):
-            c0, c1, b0, b1, x0, x1 = 64 * h, 64 * h + 64, 4 * h, 4 * h + 4, 1024 * h, 1024 * h + 1024
-            oi, oe = R("OI", b0, b1), R("OE", b0, b1)
-            return {
-                "SG": lambda: ts(R("SG", c0, c1), R(dbank[h], 0, 64), -16384.0, A.max, 16384.0, A.min),
-                "S1": lambda: scan(R("S1", c0, c1), R("D0", c0, c1), R("SG", c0, c1), 0.0, A.max, A.subtract),
-                "S2": lambda: scan(R("S2", c0, c1), R("C128", c0, c1), R("S1", c0, c1), 0.0, A.add, A.max),
-                "K": lambda: tt(R("K", b0, b1), R("S2", c0 + 15, c1, 16), R("BOFF", b0, b1), A.subtract),
-                "A1": lambda: ts(R("A1", b0, b1), R("K", b0, b1), 127, A.bitwise_and),
-                "OI": lambda: ts(oi, R("A1", b0, b1), col(CA), A.add, -64.0 * h, A.add),
-                "A2": lambda: ts(R("A2", b0, b1), R("K", b0, b1), 7, A.logical_shift_right, 127, A.bitwise_and),
-                "OE": lambda: ts(oe, R("A2", b0, b1), -1.0, A.mult, col(CE + h), A.add),
-                "MK": lambda: cp((R("MK", x0, x1), oi), R("ZR", 0, 64)),
-                "SC": lambda: scan(R("SC", x0, x1), R("MK", x0, x1), R("X", x0, x1), 0.0, A.mult, A.max),
-                "GX": lambda: act(R("GX", c0, c1), (R("X", x0, x1), oi), F.Copy),
-                "GD": lambda: act(R("GD", c0, c1), (R("DV", x0, x1), oi), F.Copy),
-                "MM": lambda: act(R("MM", c0, c1), (R("SC", x0, x1), oe), F.Copy),
-                "Z2": lambda: tt(R("Z2", c0, c1), (R("SC", x0, x1), oe), R("ZZ", c0, c1), A.add),
-            }
-
-        halves = {}
-        for h in range(2):
-            for nm, fn in half(h).items():
-                halves[nm + "ab"[h]] = fn
-
-        for tk in PLAN:
-            kind = tk[0]
-            if kind == "f":
-                fill[tk[1]]()
-            elif kind == "t":
-                halves[tk[1]]()
-            elif kind == "i":
-                if t == 1 and tk[1:] == ("v", 0):
-                    tt(R("TQ"), (R("CUT"), R("CL")), R("EL", 0, 128), A.mult)
-                    tt(vq, R("TQ"), R("EL", 128, 256), A.add)
-                ix[tk[1]][tk[2]]()
-                if t == 0 and tk[1] == "v":
-                    late[tk[2]]()
-                    if tk[2] == 2:
-                        late[3]()
-                        late[4]()
-            elif kind == "preC":
-                mm(R("B5", 0, 128), R("I32"), P_(t), True, False)
-                mm(R("B5", 0, 128), R("NI32"), C_(t), False, False)
-                mm(R("B6", 0, 128), R("I32"), C_(t), True, False)
-                if qsel:
-                    mm(R("B3", 0, 128), R("I32"), C_(t), True, False)
-            elif kind == "preQ":
-                if qsel:
-                    mm(R("B3", 0, 128), R("NI32"), vq, False, False)
-                    mm(R("B4", 0, 128), R("I32"), vq, True, False)
-            else:
-                s_, a0, a1 = tk[1], tk[2], tk[3]
-                lo, hi = 128 * a0, 128 * a1
-                dd, aa = ("DY", "AY") if s_ == "y" else ("DV", "AV")
-                lst = (R("TAB", 0, 2048 + EXT), R("I" + s_.upper(), 8 * a0, 8 * a1))
-                one, two, lin = ("EBN", "EB2N", "EBP") if s_ == "y" else ("EBP", "EB2P", "EBN")
-                if kind == "X":
-                    act(R("X", lo, hi), lst, F.Copy)
-                elif kind == "W":
-                    cp(R("X", lo, hi), lst)
-                elif kind == "d":
-                    tt(R(dd, lo, hi), lst, R("X", lo, hi), A.subtract)
-                elif kind == "l":
-                    for a in range(a0, a1):
-                        dsum(a, dd, lin)
-                elif kind == "r":
-                    ts(R(aa, lo, hi), R(dd, lo, hi), 0.0, A.max)
-                    for a in range(a0, a1):
-                        dsum(a, aa, two)
-                elif kind == "b":
-                    act(R(aa, lo, hi), R(dd, lo, hi), F.Abs)
-                    for a in range(a0, a1):
-                        dsum(a, aa, one)
-                elif kind == "g":
-                    act(R(dd, lo, hi), lst, F.Copy)
-                    mm(R(tk[4], 0, hi - lo), R("NIB"), R("X", lo, hi), True, False)
-                    mm(R(tk[4], 0, hi - lo), R("IB"), R(dd, lo, hi), False, True)
-                elif kind == "c":
-                    act(R(aa, lo, hi), R(tk[4], 0, hi - lo), F.Abs)
-                    for a in range(a0, a1):
-                        dsum(a, aa, one)
-        if not last:
-            u_pre()
-        oc = R("OC0") if t == 0 else R("OC")
-        thr = col(CTHR) if t == 0 else col(THR)
-        um = R("SU", 15, 128, 16)
-        x3 = idx_steps(C_(t + 1), "x")
-
-        def m_s():
-            mm(R("B7", 0, 128), R("I2B"), R("GX"), True, False)
-            for j in plain_v:
-                for a in (2 * (j % 8), 2 * (j % 8) + 1):
-                    lanes = (64 * (j // 8) + a, 64 * (j // 8) + 64, 16)
-                    mm(R("B7", *lanes), R("NIB"), R("GX", *lanes), False, False)
-            mm(R("B7", 0, 128), R("IB"), R("GD"), False, True)
-
-        def new_q():
-            act(R("QO"), R("B4", 0, 128), F.Copy)
-            if last:
-                store("s", "yq", R("QO"))
-            else:
-                send(t + 1)
-
-        def code():
-            cp(oc, R("CD"))
-            if t == 0:
-                send(1)
-
-        def new_c():
-            act(C_(t + 1), R("B6", 0, 128), F.Copy)
-            if last:
-                store("s", "yc", C_(t + 1))
-
-        def new_table():
-            cp((R("TAB"), R("OT", 0, 8 if last else 11)), R("VAL", 0, 128 if last else 176))
-            if last:
-                store("s", "yx", R("TAB", 0, 2048))
-
-        def new_marks():
-            if last:
-                act(R("YZ"), R("B7", 0, 128), scale=0.5, bias=-1024.0)
-                store("a", "yz", R("YZ"))
-            else:
-                act(R("ZZ"), R("B7", 0, 128), scale=0.5, bias=1023.5)
-
-        def new_p():
-            act(P_(t + 1), (R("POOL", 0, 512), R("OR")), F.Copy)
-            if last:
-                store("a", "yp", P_(t + 1))
-
-        def new_pool():
-            cp((R("POOL"), R("OP")), C_(t + 1))
-            store("a", "yl", R("POOL", 0, 512))
-
-        step = {
-            "S": lambda: ts(R("S"), R("K"), thr, A.subtract, -1.0, A.max),
-            "CD": lambda: ts(R("CD"), R("S"), 0x78F, A.bitwise_and),
-            "OC": code,
-            "PS": fill[4],
-            "NN": lambda: ts(R("NN"), R("S"), 0.0, A.is_lt, 512.0, A.mult),
-            "CT": lambda: act(R("CT"), (R("CUT"), oc), F.Copy),
-            "mQ1": lambda: mm(R("B3", 0, 128), R("I4K"), R("CT"), False, True),
-            "mQ2": lambda: mm(R("B4", 0, 128), R("IN2K"), R("CT"), False, False),
-            "mC1": lambda: mm(R("B5", 0, 128), R("I4K"), R("CT"), False, True),
-            "mC2": lambda: mm(R("B6", 0, 128), R("IN2K"), R("CT"), False, False),
-            "RQ": lambda: act(R("RQ"), R("B3", 0, 128), F.Relu, bias=-2048.0),
-            "RC": lambda: act(R("RC"), R("B5", 0, 128), F.Relu, bias=-2048.0),
-            "mQ3": lambda: mm(R("B4", 0, 128), R("I32"), R("RQ"), False, True),
-            "mC3": lambda: mm(R("B6", 0, 128), R("I32"), R("RC"), False, True),
-            "QO": new_q,
-            "CN": new_c,
-            "mS": m_s,
-            "FS": lambda: act(R("FS"), R("B7", 0, 128), scale=0.4995, bias=MAG),
-            "VAL": lambda: act(R("VAL", 0, 128), R("FS"), bias=-MAG),
-            "VAL2": lambda: act(R("VAL", 128, 176), R("FS", 0, 48), bias=-MAG),
-            "IO": lambda: iota(R("MK"), [[0, 2048]], 1, 0),
-            "mU": u_main,
-            "mM0": lambda: mm(R("B0", 0, 128), R("IB"), R("MKD"), True, False),
-            "mM": lambda: mm(R("B0", 0, 128), R("WB"), R("MM"), False, True),
-            "SU": lambda: scan(R("SU"), R("RS"), R("B0", 0, 128), -8388608.0, A.add, A.max),
-            "F16": lambda: ts(R("F16"), um, MAG4, A.add, MAG4, A.subtract),
-            "T2": lambda: tt(R("T2"), um, R("BT"), A.add),
-            "AT": lambda: tt(R("AT"), R("T2"), R("F16"), A.subtract),
-            "OT": lambda: cp(R("OT", 0, 8), R("AT")),
-            "OT2": lambda: ts(R("OT", 8, 11), R("AT", 0, 3), 2048.0, A.add),
-            "TAB": new_table,
-            "KI": lambda: ts(R("KI"), um, 7.5, A.add),
-            "A511": lambda: ts(R("A511"), R("KI"), 511, A.bitwise_and),
-            "OR": lambda: cp(R("OR"), R("A511")),
-            "PN": new_p,
-            "FU": lambda: ts(R("FU"), U1, MAG11, A.add, MAG11, A.subtract),
-            "UU": lambda: tt(U2, U2, R("FU"), A.subtract),
-            "x0": x3[0], "x1": x3[1], "x2": x3[2],
-            "mZ": lambda: mm(R("B7", 0, 128), R("I16"), R("Z2"), True, True),
-            "ZZ": new_marks,
-            "mN": lambda: mm(R("B5", 0, 8), R("ONESB"), R("NN"), True, True),
-            "CJ": lambda: act(R("CJ"), R("B5", 0, 8), scale=1.0 / 512, accum=col(CNT)),
-            "c1": lambda: act(col(CF1), col(CNT), scale=0.4999, bias=MAG),
-            "c2": lambda: act(col(CB1), col(CNT), scale=16384.0, bias=col(CTHR)),
-            "c3": lambda: act(col(CF2), col(CF1), bias=-MAG),
-            "c4": lambda: act(col(THR), col(CF2), scale=-32768.0, bias=col(CB1)),
-            "A3": lambda: ts(R("A3"), R("KI"), 3, A.bitwise_and),
-            "NB": lambda: tt(R("NB"), R("NN"), R("BP"), A.add),
-            "AP": lambda: tt(R("AP"), R("A3"), R("NB"), A.add),
-            "OP": lambda: cp(R("OP"), R("AP")),
-            "PL": new_pool,
-        }
-        step.update(halves)
-        for nm in (CUTS + " " + (LAST if last else TAIL)).split():
-            if qsel or nm not in ("mQ1", "mQ2", "RQ", "mQ3", "QO"):
-                step[nm]()
-
+        mark[i] = (s, cnt[s])
     for s in sorted(cnt):
         g.wait_ge(T.sem[s], cnt[s])

from concourse.bass import DstId, RemoteDMATransfer
from concourse.mybir import dt, AluOpType, AxisListType, ActivationFunctionType

A = AluOpType
F = ActivationFunctionType
VIS = 6
EXT = 560
MAG = 12582912.0
LIFT = 1056.0
NBS = (4, 4)
PLAN = ([("x", "a", 0, 9), ("x", "v", 9, 16), ("y", "S", 0, 8), ("y", "S", 8, 15), ("y", "M", 15, 16),
         ("v", "V", 0, 8), ("v", "V", 8, 16)],
        [("x", "a", 0, 8), ("x", "a", 8, 16), ("y", "S", 0, 8), ("y", "S", 8, 16),
         ("v", "V", 0, 3), ("v", "M", 3, 8), ("v", "V", 8, 10), ("v", "V", 10, 16)])
RANK = {"lx": (-77, -76), "ly": (-112, -47), "lv": (-35, -95), "x": (-30, 16), "y": (6, 22), "v": (-15, 69),
        "cut": (-92, 13), "rec": (35, 16), "max": (80, -4), "place": (4, 43), "val": (122, 53), "tab": (248, -5),
        "mark": (-89, 19), "pool": (160, 108), "count": (92,), "child": (38, 53)}
QUICK = (True, False)
LAST = {"x": (-33, 8), "y": (-24, 33), "v": (-33, 65), "pool": (140, 100), "mark": (38, 93), "max": (25, -33),
        "place": (36, 1), "val": (33, 43), "tab": (18, 49), "cut": (-68, -2), "rec": (11, 33)}
CY, WAKE, GATHER, SCATTER, PECY, DMA0, DMAB, HOP, SLACK = 0.00087, 0.15, 1.3, 2.8, 0.00048, 1.6, 0.00032, 3.75, 0.03
NEAR, ROWS = 0.15, 0.4
ON = dict([(n, "v") for n in "NNb Iva Ivb OOa OCa DQa GDa CFa".split()]
          + [(n, "a") for n in "Ixa Ixb Iya Iyb OOb OCb CTb KCa GXb GDb VALa VALb MMb Pa Pb Za FUa FUb CFa1".split()])
FIRST = {"lx": (-75, -59), "ly": (-77, -26), "lv": (-56, -24), "x": (-58, -52), "y": (-43, 25), "v": (16, 85),
         "rec": (49, 28)}
LATER = -0.5
CH = range(len(NBS))
INHERIT = False
LONG, SOON, FIT, PIECES = 0.15, 0.07, 0.03, (1, 1)

SCRATCH = {}
SIZE = {"float32": 4, "int32": 4, "bfloat16": 2, "float16": 2, "uint16": 2}


def _decl(names, cols, dtype, where="sbuf"):
    for n in names.split():
        SCRATCH[n] = (where, [128, cols], dtype)


_decl("X DV DY AV AY SC MK CUT", 2048, "bfloat16")
_decl("TAB", 2048 + 768, "bfloat16")
_decl("POOL POOL2", 1536, "float32")
_decl("PLI", 512, "int32")
_decl("S1_ S2_ S3_ S4_ S5_", 384, "float16")
_decl("S6_", 384, "float32")
_decl("V1 V2 V3 V4 V5 P0 FU I16 NI16 IH16 N2K CN Z WS W16 WN DQ TQ", 128, "float16")
_decl("EAR EL KEEP", 256, "float16")
_decl("CI PI_ QI Hx Hy Hv Gx Gy Gv VAL SU", 128, "int32")
_decl("ZB ZR IB NIB IH NIH I4K N4K GX GD CT CTV MM WB MKD C32 ONE", 128, "bfloat16")
_decl("G KP D0 C128 SG S1 S2 RS", 128, "float32")
_decl("GE", 144, "float32")
_decl("EBP EBN EB2P EB2N", 144, "bfloat16")
_decl("Ix Iy Iv", 128, "uint16")
_decl("PERM0 PERM1 OC0 OC1 OD0 OD1 CL0 CL1", 8, "uint16")
_decl("OO0 OO1", 16, "uint16")
_decl("OL0 OL1", 24, "uint16")
_decl("KK0 KK1 AA0 AA1", 16, "int32")
_decl("AT0 AT1", 24, "int32")
_decl("OFF0 OFF1", 24, "float16")
_decl("CD PA", 8, "int32")
_decl("B8 BOFF BT PW", 8, "float32")
_decl("NN", 8, "bfloat16")
_decl("LE GEP", 16, "float32")
_decl("WI DI", 4, "int32")
_decl("PN", 2, "int32")
_decl("CF", 24, "float32")
_decl("BD0 BD1 BF0 BF1 BG1 BG2 BU0 BU1", 512, "float32", "psum")

LOADS = ["wt", "zt", "ch", "pa", "de", "vi", "pl", "xt", "x2"]
NMSG = 1 + len(NBS) * (VIS - 1)
SEMAPHORES = ["sv", "sa", "sp", "sg", "ls", "out"] + ["l_" + n for n in LOADS] + ["m%d" % i for i in range(NMSG)]

PF, KF, G16, C37, C16, C4, WF, WG, CTHR, THR, CF1, CF2, UB, C4P, CA = range(15)
B0 = (0, NBS[0])
LANES = [(16 * B0[h], 16 * (B0[h] + NBS[h])) for h in CH]


def message(i):
    if i == 0:
        return ("EAR", 0, 256), ("EL", 0, 256)
    t, h = divmod(i - 1, len(NBS))
    c0, c1 = LANES[h]
    if t == 0:
        return ("OD%d" % h, 0, 8), ("CL%d" % h, 0, 8)
    return ("S%d_" % (t + 1), 3 * c0, 2 * c0 + c1), ("V%d" % (t + 1), c0, c1)


def route(T, topo, r):
    src = T.cores[r]
    dst = T.cores[(r + 1) % len(T.cores)]
    if topo.may_write(src, dst):
        return [src, dst]
    cand = [c for c in topo.cores_of(src) if c != src and T.rank_of(c) is None and topo.may_write(c, dst)]
    near = [c for c in cand if topo.die(c) == topo.die(src)]
    return [src, (near or cand)[0], dst]


def R(n, lo=0, hi=None, st=None):
    if hi is None:
        hi = SCRATCH[n][1][1]
    return (n, lo, hi) if st is None else (n, lo, hi, st)


def col(c):
    return ("CF", c, c + 1)


def width(r):
    if isinstance(r[0], tuple):
        return 16 * width(r[1])
    return len(range(*r[1:]))


def program():
    calls = []
    rank = [-10000]

    def stage(name, t, h=0):
        rank[0] = 100 * t + {0: FIRST, VIS - 1: LAST}.get(t, {}).get(name, RANK[name])[h]
        now[:] = [t, h]

    now, label, met = [], [], {}

    def tag(out):
        if not now:
            return None
        base = (label.pop() if label else (out[0][0] if isinstance(out[0], tuple) else out[0]).rstrip("01")) + "ab"[now[1]]
        k = met[now[0], base] = met.get((now[0], base), -1) + 1
        return now[0], base + (str(k) if k else "")

    def put(e, kind, args, outs, ins, cost, after=()):
        rd, wr = [], []
        for x in ins:
            if isinstance(x, tuple):
                rd += [x[0][:3], x[1][:3]] if isinstance(x[0], tuple) else [x[:3]]
        for x in outs:
            if isinstance(x[0], tuple):
                wr.append(x[0][:3])
                rd.append(x[1][:3])
            else:
                wr.append(x[:3])
        calls.append((e, kind, args, rd, wr, cost, list(after), rank[0], tag(outs[0]) if e in "vaf" and outs else None))
        return len(calls) - 1

    def cyc(out, ins, rate=1.0):
        if isinstance(out[0], tuple):
            return 0.05 + SCATTER * width(out) * CY
        if isinstance(ins[0][0], tuple):
            return 0.06 + GATHER * width(out) * CY
        return 0.06 + rate * width(out) * CY

    def fast(*x):
        return 0.5 if all(not isinstance(r[0], tuple) and SIZE[SCRATCH[r[0]][2]] == 2 for r in x) else 1.0

    def cp(out, in_):
        put("v", "cp", (out, in_), [out], [in_], cyc(out, [in_], fast(out, in_)))

    def tt(out, a, b, alu):
        both = not isinstance(a[0], tuple) and SCRATCH[a[0]][0] == SCRATCH[b[0]][0]
        put("v", "tt", (out, a, b, alu), [out], [a, b], cyc(out, [a], 2.0 if both else 1.0))

    def ts(out, a, s1, o0, s2=None, o1=None):
        put("v", "ts", (out, a, s1, s2, o0, o1), [out], [a, s1, s2], cyc(out, [a], fast(out, a)))

    def scan(out, d0, d1, init, o0, o1):
        put("v", "scan", (out, d0, d1, init, o0, o1), [out], [d0, d1], cyc(out, [d0], fast(out, d0, d1)))

    def mset(out, v):
        put("v", "mset", (out, v), [out], [], cyc(out, [out], fast(out)))

    def act(out, in_, func=F.Identity, bias=0.0, scale=1.0):
        put("a", "act", (out, in_, func, bias, scale), [out], [in_, bias, scale], cyc(out, [in_]))

    def lin(out, in_, scale=1.0, bias=0.0, relu=False, on="f"):
        if relu and SCRATCH[out[0]][2] != "uint16":
            v = ("ts", (out, in_, bias, 0.0, A.add, A.max) if scale == 1.0 else (out, in_, scale, 0.0, A.mult, A.max))
        elif scale == 1.0:
            v = ("cp", (out, in_)) if bias == 0.0 else ("ts", (out, in_, bias, None, A.add, None))
        else:
            v = ("ts", (out, in_, scale, bias, A.mult, A.add))
        func = F.Relu if relu else F.Copy if (scale, bias) == (1.0, 0.0) else F.Identity
        ways = {"v": v + (cyc(out, [in_], fast(out, in_)),), "a": ("act", (out, in_, func, bias, scale), cyc(out, [in_]))}
        if on == "f":
            put("f", "either", ways, [out], [in_, bias, scale], ways["a"][2])
        else:
            put(on, ways[on][0], ways[on][1], [out], [in_, bias, scale], ways[on][2])

    def whole(out, in_, tmp, on):
        if on == "v":
            ts(out, in_, MAG, A.add, MAG, A.subtract)
        else:
            act(tmp, in_, bias=MAG)
            lin(out, tmp, bias=-MAG)

    def mm(out, lhs, rhs, start, stop):
        put("p", "mm", (out, lhs, rhs, start, stop), [out], [lhs, rhs], max(64, width(rhs)) * PECY)

    def group(*terms):
        for i, (o, l, r) in enumerate(terms):
            mm(o, l, r, i == 0, i == len(terms) - 1)

    def iota(out, pat, base, cm, after=()):
        put("g", "iota", (out, pat, base, cm), [out], [], 0.13 + 2 * width(out) * CY, after)

    def load(e, name, out, lo=0, ins=(), sem=None):
        put(e, "load", (out, name, lo, "l_" + (sem or name)), [out], ins, width(out) * SIZE[SCRATCH[out[0]][2]] * DMAB)

    def store(e, name, lo, in_):
        put(e, "store", (in_, name, lo), [], [in_], width(in_) * SIZE[SCRATCH[in_[0]][2]] * DMAB)

    def send(i):
        s, d = message(i)
        k = put("g", "send", (i,), [], [s], 0.3)
        put("r", "land", (i,), [d], [], HOP, [k])
        return k

    load("s", "wt", R("WI", 0, 1))
    load("a", "zt", R("ZB"))
    load("s", "ch", R("CI"))
    load("a", "xt", R("TAB", 0, 2048))
    load("s", "pa", R("PI_"))
    load("s", "vi", R("QI"))
    load("s", "de", R("DI", 0, 1))
    load("s", "pl", R("PLI"), ins=[R("TAB", 0, 2048)])
    iota(R("PN", 0, 1), [[0, 1]], 0, 1)
    iota(R("GE"), [[1, 144]], -16, 0)
    iota(R("B8"), [[1, 8]], 0, 0)
    iota(R("G"), [[16, 8], [0, 16]], 0, 0)
    iota(R("KP"), [[0, 8], [1, 16]], 0, 0)
    for c0, c1 in LANES:
        iota(R("MK", 16 * c0, 16 * c1), [[0, 16 * (c1 - c0)]], 1, 0)
    mset(R("ZR"), 0.0)
    mset(R("C32"), 32.0)
    mset(R("C128"), 128.0)
    act(R("CN"), R("ZR"), bias=-LIFT)
    mset(R("ONE"), 1.0 / 512)
    ts(R("PN", 1, 2), R("PN", 0, 1), 15, A.bitwise_and)
    mset(R("OD0"), 0)
    mset(R("OD1"), 0)
    cp(R("CF", PF, KF + 1), R("PN"))
    ts(R("IB"), R("GE", 16, 144), col(PF), A.is_equal)
    tt(col(G16), col(PF), col(KF), A.subtract)
    mset(R("CUT"), -1.0)
    act(col(C16), col(KF), scale=16.0)
    act(col(C37), col(KF), scale=37.0)
    act(col(C4), col(KF), scale=4.0)
    act(col(C4P), col(KF), scale=4.0, bias=512.0)
    act(R("N2K"), R("IB"), scale=-2048.0)
    for h in CH:
        nb = NBS[h]
        act(R("OFF%d" % h, 0, nb), R("B8", 0, nb), scale=256.0, bias=col(C16))
        act(R("OFF%d" % h, nb, 2 * nb), R("ZR", 0, nb))
        act(R("OFF%d" % h, 2 * nb, 3 * nb), R("B8", 0, nb), scale=64.0, bias=col(C4 if h else C4P))
        act(col(CA + h), col(KF), scale=16.0 * nb, bias=-16.0 * B0[h])
    for nb in sorted(set(NBS)):
        q16 = R("OFF%d" % NBS.index(nb), 0, nb)
        ts(R("PA", 0, nb), q16, 1.0 / (16 * nb), A.mult, 0.5 / nb - 0.5, A.add)
        act(R("PW", 0, nb), R("PA", 0, nb), scale=1.0 - 16 * nb)
        tt(R("PERM%d" % NBS.index(nb), 0, nb), R("PW", 0, nb), q16, A.add)
    ts(R("EBP"), R("GE"), col(G16), A.is_equal, 16384.0, A.mult)
    for name, scale in (("I16", 1.0), ("NIB", -1.0), ("NI16", -1.0), ("IH16", 0.5)):
        act(R(name), R("IB"), scale=scale)
    cp(col(WF), R("WI", 0, 1))
    ts(col(WG), R("WI", 0, 1), 1.0 / 2048, A.mult)
    ts(R("GEP"), R("KP", 0, 16), col(KF), A.add, 15.0, A.is_ge)
    ts(R("WS"), R("G"), col(G16), A.is_equal, col(WG), A.mult)
    ts(R("W16"), R("G"), col(G16), A.is_equal, col(WF), A.mult)
    act(R("Z"), R("ZB"), bias=LIFT)
    group((R("BD0", 0, 1), R("WS"), R("CN", 0, 1)))
    lin(col(UB), R("BD0", 0, 1), bias=LIFT - 2047.0 / 4096)
    ts(R("LE"), R("KP", 0, 16), col(KF), A.is_ge)
    tt(R("WN"), R("W16"), R("N2K"), A.add)
    rank[0] = LATER
    for name, scale in (("EBN", -1.0), ("EB2P", 2.0), ("EB2N", -2.0)):
        act(R(name), R("EBP"), scale=scale)
    act(R("D0"), R("G"), scale=32641.0, bias=30720.0)
    ts(R("MKD"), R("KP"), col(KF), A.not_equal, -4194304.0, A.mult)
    ts(R("RS"), R("KP"), 0.0, A.is_equal, -8388608.0, A.mult)
    for j in range(16):
        lin(R("CUT", 128 * j + 112, 128 * j + 128), R("GEP"), R("LE", j, j + 1), -1.0, on="vva"[j % 3])
    tt(R("D0"), R("D0"), R("KP"), A.add)
    act(R("WB"), R("W16"))
    for name, scale in (("IH", 0.5), ("NIH", -0.5), ("I4K", 4096.0), ("N4K", -4096.0)):
        act(R(name), R("IB"), scale=scale)

    def seq(s, t, h):
        c0, c1 = LANES[h]
        if t == 0:
            return {"x": R("EAR", c0, c1), "y": R("P0", c0, c1), "v": R("EAR", 128 + c0, 128 + c1)}[s]
        if s == "v":
            return R("V%d" % t, c0, c1)
        k = 3 * c0 + "qxy".index(s) * (c1 - c0)
        return R("S%d_" % t, k, k + c1 - c0)

    def u_of_marks(h):
        c0, c1 = LANES[h]
        n = c1 - c0
        u1, u2 = R("BU%d" % h, 128, 128 + n), R("BU%d" % h, 0, n)
        group((u1, R("WS"), R("Z", c0, c1)))
        lin(R("FU", c0, c1), u1, bias=col(UB))
        group((u2, R("IB"), R("C32", 0, n)), (u2, R("WN"), R("CN", 0, n)), (u2, R("W16"), R("Z", c0, c1)),
              (u2, R("N2K"), R("FU", c0, c1)))

    def lists(s, t, h):
        c0, c1 = LANES[h]
        stage("l" + s, t, h)
        tt(R("H" + s, c0, c1), R("BU%d" % h, 0, c1 - c0), seq(s, t, h), A.mult)
        ts(R("G" + s, c0, c1), R("H" + s, c0, c1), 5, A.logical_shift_right, 2047, A.bitwise_and)
        lin(R("I" + s, c0, c1), (R("G" + s, c0, c1), R("PERM%d" % NBS.index(NBS[h]), 0, NBS[h])), bias=col(C37))

    def select(h, ct, keep, take, out, name="C"):
        n, m = width(ct), width(out)
        parts = range(0, m, n)
        first = [] if m == n else [(R("BG1", 0, m), R("ZR"), R("CUT", 0, m))]
        group(*(first + [(R("BG1", k, k + n), R("I16"), keep[k // n]) for k in parts]
                + [(R("BG1", k, k + n), R("N4K"), ct) for k in parts]))
        group(*([(R("BG2", 0, m), R("I16"), take)] + [(R("BG2", k, k + n), R("I4K"), ct) for k in parts]))
        kept = R("KEEP", 2 * LANES[h][0], 2 * LANES[h][0] + m)
        label.append("K" + name)
        lin(kept, R("BG1", 0, m), bias=-4096.0, relu=True)
        label.append(name)
        tt(out, R("BG2", 0, m), kept, A.max)

    bank = [0]

    def gathers(t, h, which):
        nb = NBS[h]
        c0, c1 = LANES[h]
        w = 16 * nb
        sums = R("BD%d" % h, 0, w)

        def dsum(a0, a1, buf, eb):
            for a in range(a0, a1):
                lo = 16 * c0 + w * a
                lhs, rhs = R(eb, 16 - a, 144 - a), R(buf, lo, lo + w)
                put("p", "sum", (sums, lhs, rhs, (t, h)), [sums], [lhs, rhs], max(64, w) * PECY)

        for s, way, a0, a1 in PLAN[h]:
            lo, hi = 16 * c0 + w * a0, 16 * c0 + w * a1
            lst = (R("TAB", 0, 2048 + EXT), R("I" + s, lo // 16, hi // 16))
            xs = R("X", lo, hi)
            stage(s, t, h)
            if s not in which:
                continue
            if s == "x":
                lin(xs, lst, on=way)
                continue
            dd, aa = ("DY", "AY") if s == "y" else ("DV", "AV")
            one, two, neg = ("EBN", "EB2N", "EBP") if s == "y" else ("EBP", "EB2P", "EBN")
            if way == "S":
                act(R(dd, lo, hi), lst, F.Copy)
                df = R("BF%d" % (bank[0] % 2), 0, hi - lo)
                bank[0] += 1
                group((df, R("NIB"), xs), (df, R("IB"), R(dd, lo, hi)))
                act(R(aa, lo, hi), df, F.Abs)
                dsum(a0, a1, aa, one)
                continue
            tt(R(dd, lo, hi), lst, xs, A.subtract)
            if way == "V":
                dsum(a0, a1, dd, neg)
                ts(R(aa, lo, hi), R(dd, lo, hi), 0.0, A.max)
                dsum(a0, a1, aa, two)
            else:
                act(R(aa, lo, hi), R(dd, lo, hi), F.Abs)
                dsum(a0, a1, aa, one)

    def cut(t, h):
        last = t == VIS - 1
        nb, b0 = NBS[h], B0[h]
        c0, c1 = LANES[h]
        n, x0, x1 = c1 - c0, 16 * c0, 16 * c1
        ln = lambda name: R(name, c0, c1)
        bl = lambda name: R(name, b0, b0 + nb)
        own = lambda name, k0, k1: R("%s%d" % (name, h), k0 * nb, k1 * nb)
        stage("cut", t, h)
        ts(ln("SG"), R("BD%d" % h, 0, n), -16384.0, A.max, 16384.0, A.min)
        scan(ln("S1"), ln("D0"), ln("SG"), 0.0, A.max, A.subtract)
        scan(ln("S2"), ln("C128"), ln("S1"), 0.0, A.add, A.max)
        end = R("S2", c0 + 15, c1, 16)
        tt(own("KK", 0, 1), end, bl("BT" if t else "BOFF"), A.subtract)
        lin(own("KK", 1, 2), end, -1.0 / 128, -129.0 / 256)
        ts(own("AA", 0, 2), own("KK", 0, 2), 127, A.bitwise_and)
        lin(own("OO", 0, 2), own("AA", 0, 2), bias=col(CA + h))
        oi, oe = own("OO", 0, 1), own("OO", 1, 2)
        stage("rec", t, h)
        ts(bl("CD"), own("KK", 0, 1), 0x8078F, A.bitwise_and)
        oc = own("OD" if t == 0 else "OC", 0, 1)
        label.append("OC")
        lin(oc, bl("CD"), -1.0, 2047.0, relu=True)
        sent = send(1 + h) if t == 0 else None
        x, y, q = seq("x", t, h), seq("y", t, h), seq("q", t + 1, h)
        short = QUICK[h] and 0 < t < VIS - 1
        if short:
            group((R("BG1", 0, n), R("I16"), x), (R("BG1", 0, n), R("NI16"), seq("v", t, h)))
            lin(ln("DQ"), R("BG1", 0, n))
            tt(ln("TQ"), (R("CUT"), oc), ln("DQ"), A.mult)
            label.append("Q")
            tt(q, ln("TQ"), x, A.add)
            sent = send(1 + len(NBS) * t + h)
            stage("child", t, h)
        lin(ln("CT"), (R("CUT"), oc))
        if t == 0 or short:
            select(h, ln("CT"), [x], y, seq("x", t + 1, h))
        else:
            select(h, ln("CT"), [seq("v", t, h), x], (x[0], x[1], y[2]), (q[0], q[1], q[2] + n))
            if last:
                store("s", "yq", c0, q)
                store("s", "yc", c0, seq("x", t + 1, h))
            else:
                sent = send(1 + len(NBS) * t + h)
        stage("val", t, h)
        nn, cd = bl("NN"), bl("CD")
        put("f", "either", {"v": ("ts", (nn, cd, 524288.0, 512.0, A.is_ge, A.mult), cyc(nn, [cd])),
                            "a": ("act", (nn, cd, F.Relu, -2.0, 513.3 / 524288), cyc(nn, [cd]))}, [nn], [cd], cyc(nn, [cd]))
        lin(ln("GX"), (R("X", x0, x1), oi))
        lin(ln("GD"), (R("DV", x0, x1), oi))
        val = R("BF0" if h == CH[-1] else "BD0", 0, n)
        plain = [(16 * b + a0, 16 * b + a1) for s, way, a0, a1 in PLAN[h] if s + way == "vS" for b in range(nb)]
        group(*([(val, R("IB"), ln("GX"))]
                + [(R(val[0], lo, hi), R("NIH"), R("GX", c0 + lo, c0 + hi)) for lo, hi in plain]
                + [(val, R("IH"), ln("GD"))]))
        lin(ln("VAL"), val, bias=-0.25)
        stage("max", t, h)
        cp((R("MK", x0, x1), oi), R("ZR", 0, n))
        step = (x1 - x0) // PIECES[h]
        for k in range(x0, x1, step):
            scan(R("SC", k, k + step), R("MK", k, k + step), R("X", k, k + step), 0.0, A.mult, A.max)
        lin(ln("MM"), (R("SC", x0, x1), oe))
        um = R("BD%d" % h, 0, n)
        group((um, R("IB"), ln("MKD")), (um, R("WB"), ln("MM")))
        scan(ln("SU"), ln("RS"), um, -8388608.0, A.add, A.max)
        stage("place", t, h)
        for k, mask in enumerate((15, 511, 3)):
            ts(own("AT", k, k + 1), R("SU", c0 + 15, c1, 16), mask, A.bitwise_and)
        off = "BF1" if h == CH[-1] else "BD0"
        group((R(off, 0, 3 * nb), R("I16"), own("OFF", 0, 3)),
              (R(off, 2 * nb, 3 * nb), R("IB" if h else "NIB"), bl("NN")))
        tt(own("OL", 0, 3), R(off, 0, 3 * nb), own("AT", 0, 3), A.add)
        label.append("P")
        lin(seq("y", t + 1, h), (R("POOL", 512, 1024), own("OL", 1, 2)))
        stage("mark", t, h)
        zp = R("BU%d" % h, 256, 256 + n)
        group((zp, R("IH16"), ln("Z")), (zp, R("IH"), ln("MM")))
        lin(ln("Z"), zp, bias=LIFT / 2 - 0.25)
        if last:
            store("s", "yp", c0, seq("y", t + 1, h))
            lin(ln("ZB"), ln("Z"), bias=-LIFT)
            store("s", "yz", c0, ln("ZB"))
        else:
            u_of_marks(h)
        return sent

    def writes(t, h):
        last = t == VIS - 1
        nb = NBS[h]
        c0, c1 = LANES[h]
        stage("tab", t, h)
        cp((R("TAB", 16 * c0, 16 * c1), R("OL%d" % h, 0, nb)), R("VAL", c0, c1))
        if last:
            store("s", "yx", 16 * c0, R("TAB", 16 * c0, 16 * c1))
        elif h == 0:
            cp((R("TAB", 2048, 2048 + 768), R("OL0", 0, 3)), R("VAL", 0, 48))

    def pool_writes(t, h):
        nb = NBS[h]
        c0, c1 = LANES[h]
        stage("pool", t, h)
        pool = "POOL2" if t == VIS - 1 else "POOL"
        win = R(pool, 512 + 4 * c0, 1536) if h else R(pool, 0, 512 + 4 * c1)
        label.append("POOL")
        cp((win, R("OL%d" % h, 2 * nb, 3 * nb)), seq("x", t + 1, h))
        if t == VIS - 1:
            store("a", "yl", 4 * c0, R(pool, 512 + 4 * c0, 512 + 4 * c1))
        elif t == VIS - 2 and h == CH[-1]:
            put("s", "copy", (R("POOL2", 512, 1024), R("POOL", 512, 1024), "l_x2"), [R("POOL2", 512, 1024)],
                [R("POOL", 512, 1024)], 2048 * DMAB)

    stage("rec", 0)
    label.extend(["EXT", "PI", "QI", "CI", "BOFF", "TH"])
    lin(col(CTHR), R("DI", 0, 1), 16384.0, 16384.0)
    lin(R("BOFF"), R("B8"), 524288.0, col(CTHR))
    stage("lx", 0)
    lin(R("EAR", 0, 128), R("CI"))
    lin(R("EAR", 128, 256), R("QI"))
    lin(R("P0"), R("PI_"))
    lin(R("TAB", 2048, 2048 + EXT), R("TAB", 0, EXT), on="v")
    send(0)
    for h in CH:
        stage("lx", 0, h)
        label.append("U")
        u_of_marks(h)
        lists("x", 0, h)
        lists("y", 0, h)
    stage("rec", 0)
    label.append("PL")
    lin(R("POOL", 512, 1024), R("PLI"))
    for t in range(VIS):
        last = t == VIS - 1
        for h in CH:
            gathers(t, h, "xy")
        for h in CH:
            if t == 1:
                c0, c1 = LANES[h]
                stage("lv", t, h)
                lin(R("CTV", c0, c1), (R("CUT"), R("CL%d" % h, 0, NBS[h])))
                select(h, R("CTV", c0, c1), [R("EL", 128 + c0, 128 + c1)], R("EL", c0, c1), seq("v", 1, h), "V")
            lists("v", t, h)
            gathers(t, h, "v")
        for h in CH:
            sent = cut(t, h)
            if not last:
                lists("x", t + 1, h)
                lists("y", t + 1, h)
        for h in CH:
            writes(t, h)
        for h in CH:
            pool_writes(t, h)
        if not last:
            stage("count", t)
            for c0, c1 in LANES:
                iota(R("MK", 16 * c0, 16 * c1), [[0, 16 * (c1 - c0)]], 1, 0, [sent])
            cnt = R("BG1", 0, 1)
            group(*[(cnt, R("ONE"), R("NN", b, b + 1)) for b in range(8)])
            lin(col(CF1), cnt, 0.4999, MAG)
            lin(col(CF2), col(CF1), -32768.0, 32768.0 * MAG)
            lin(col(THR), cnt, 16384.0, col(CF2))
            lin(R("BT"), R("BOFF"), bias=col(THR))
    return calls


def needs(calls):
    acc, dep = {}, []
    for i, (e, kind, args, rd, wr, cost, after, rank, tag) in enumerate(calls):
        d = {k: calls[k][0] != e for k in after}
        for regs, w in ((rd, False), (wr, True)):
            for n, lo, hi in regs:
                bank = SCRATCH[n][0] == "psum"
                for l2, h2, w2, j in acc.get(n, []):
                    e2 = calls[j][0]
                    if bank and e == e2 == "p":
                        if not (kind == "sum" == calls[j][1] and args[3] == calls[j][2][3]):
                            d.setdefault(j, False)
                    elif (bank and (e2 != e or e == "f" or w or w2)) or (l2 < hi and lo < h2 and (w or w2)):
                        d[j] = True
        for regs, w in ((rd, False), (wr, True)):
            for n, lo, hi in regs:
                old = acc.get(n, [])
                if w and SCRATCH[n][0] == "psum":
                    old = old if kind == "sum" else []
                elif w:
                    old = [x for x in old if not (lo <= x[0] and x[1] <= hi)]
                acc[n] = old + [(lo, hi, w, i)]
        dep.append(d)
    return dep


def order(calls, dep):
    n = len(calls)
    users = [[] for _ in range(n)]
    for i in range(n):
        for j in dep[i]:
            users[j].append(i)
    rank = [c[7] for c in calls]
    for i in range(n - 1, -1, -1):
        rank[i] = min([rank[i]] + [rank[u] for u in users[i] if INHERIT])
    left, since = [len(d) for d in dep], [{q: 0.0 for q in ("va" if c[0] == "f" else c[0])} for c in calls]
    ready = [i for i in range(n) if not left[i]]
    free = {e: 0.0 for e in "vapgsrd"}
    out, span = [], 0.0
    while ready:
        at, on = {}, {}
        for i in ready:
            on[i] = calls[i][0]
            if on[i] == "f":
                on[i] = "v" if max(since[i]["v"], free["v"]) + SLACK < max(since[i]["a"], free["a"]) else "a"
                if calls[i][8] and ON.get(calls[i][8][1], "f") != "f":
                    on[i] = ON[calls[i][8][1]]
            at[i] = max(since[i][on[i]], free[on[i]])
        i = min(ready, key=lambda i: (at[i], rank[i], i))
        e = on[i]
        if calls[i][5] > LONG:
            u = min((k for k in ready if on[k] == e and at[k] <= at[i] + SOON), key=lambda k: (rank[k], at[k], k))
            fits = [k for k in ready if on[k] == e and at[k] + calls[k][5] <= at[u] + FIT]
            i = min(fits, key=lambda k: (at[k], rank[k], k)) if fits and at[u] > at[i] else u
        if calls[i][0] == "f":
            kind, args, cost = calls[i][2][e]
            calls[i] = (e, kind, args) + calls[i][3:5] + (cost,) + calls[i][6:]
        ready.remove(i)
        end = at[i] + calls[i][5]
        if calls[i][1] in ("load", "store", "copy"):
            free[e] = at[i] + 0.05
            end = free["d"] = max(free["d"], at[i] + DMA0) + calls[i][5] + ROWS
        elif e != "r":
            free[e] = end
        out.append(i)
        span = max(span, end)
        for u in users[i]:
            for q in since[u]:
                since[u][q] = max(since[u][q], end + ((NEAR if q == e else WAKE) if dep[u][i] else 0.0))
            left[u] -= 1
            if not left[u]:
                ready.append(u)
    return out, span


def places(text):
    out = {}
    for k, word in enumerate(text.split()):
        name, _, e = word.lstrip("<>").partition("@")
        out[name] = (k + 1000 * (word.count(">") - word.count("<")), e)
    return out


def listed(calls, dep, usual, final, first):
    n = len(calls)
    users = [[] for _ in range(n)]
    key = [None] * n
    for i, c in enumerate(calls):
        for j in dep[i]:
            users[j].append(i)
        place, e = {0: first, VIS - 1: final}.get(c[8][0], usual).get(c[8][1], (None, "")) if c[8] else (None, "")
        if place is not None:
            key[i] = 1000 * c[8][0] + place
        elif c[1] == "load" or c[0] in "vaf" and not c[8]:
            key[i] = c[7] + 0.001 * i
        if c[0] == "f":
            kind, args, cost = c[2][e or "a"]
            calls[i] = (e or "a", kind, args) + c[3:5] + (cost,) + c[6:]
    for i in range(n - 1, -1, -1):
        if key[i] is None:
            key[i] = min([key[u] for u in users[i]] or [1000 * VIS]) - 0.001
    for i in range(n):
        key[i] = max([key[i]] + [key[j] for j in dep[i]])
    start, end = [0.0] * n, [0.0] * n
    free = {e: 0.0 for e in "vad"}
    for i in sorted(range(n), key=lambda i: (key[i], i)):
        e, kind = calls[i][:2]
        t = max([free.get(e, 0.0)] + [end[j] + ((NEAR if calls[j][0] == e else WAKE) if w else 0.0)
                                      for j, w in dep[i].items()])
        start[i], end[i] = t, t + calls[i][5]
        if kind in ("load", "store", "copy"):
            end[i] = free["d"] = max(free["d"], t + DMA0) + calls[i][5]
        elif e in free:
            free[e] = end[i]
    return sorted(range(n), key=lambda i: (start[i], key[i], i))


PLANNED = []


def planned():
    if not PLANNED:
        calls = program()
        dep = needs(calls)
        seq = order(calls, dep)[0]
        sums = {}
        for i in seq:
            if calls[i][1] == "sum":
                sums.setdefault(calls[i][2][3], []).append(i)
        for terms in sums.values():
            for i in terms:
                calls[i] = ("p", "mm", calls[i][2][:3] + (i == terms[0], i == terms[-1])) + calls[i][3:]
        PLANNED.extend([calls, dep, seq])
    return PLANNED


def relay_program(g, core, T, topo, src, dst):
    n_in = len(topo.engines(src, core))
    n_out = len(topo.engines(core, dst))
    rid, pid = topo.addr(dst, core)
    calls, dep, seq = planned()
    for k in seq:
        if calls[k][1] == "send":
            i = calls[k][2][0]
            n, a, b = message(i)[1]
            g.wait_ge(T.sem["m%d" % i], n_in)
            g.remote_dma(T[n][:, a:b], T[n][:, a:b], T.sem["m%d" % i], T.sem.ls, pid, rid, topo.mask(core, dst))
    g.wait_ge(T.sem.ls, n_out * NMSG)


def rank_program(g, core, T, topo):
    rank = T.rank_of(core)
    nr = len(T.cores)
    if rank is None:
        for r in range(nr):
            way = route(T, topo, r)
            if len(way) == 3 and way[1] == core:
                relay_program(g, core, T, topo, way[0], way[2])
        return
    nxt = route(T, topo, rank)[1]
    prv = route(T, topo, (rank - 1) % nr)[-2]
    n_out = len(topo.engines(core, nxt))
    n_in = len(topo.engines(prv, core))
    rid, pid = topo.addr(nxt, core)
    Q = {"v": g.vector, "a": g.scalar, "p": g.tensor, "g": g, "s": g.sync}

    def ap(x):
        if not isinstance(x, tuple):
            return x
        if isinstance(x[0], tuple):
            return ap(x[0]).indirect(ap(x[1]))
        return T[x[0]][:, x[1]:x[2]:x[3]] if len(x) == 4 else T[x[0]][:, x[1]:x[2]]

    def hbm(name, lo, r):
        return T[name][:] if width(r) == T[name].shape[1] else T[name][:, lo:lo + width(r)]

    def issue(e, kind, a):
        if kind == "land":
            return "m%d" % a[0], n_in
        if kind == "send":
            s, d = message(a[0])
            g.remote_dma(ap(d), ap(s), T.sem["m%d" % a[0]], T.sem.ls, pid, rid, topo.mask(core, nxt))
            return "ls", n_out
        if kind == "load":
            Q[e].dma_start(ap(a[0]), hbm(a[1], a[2], a[0])).then_inc(T.sem[a[3]], 16)
            return a[3], 16
        if kind == "copy":
            Q[e].dma_start(ap(a[0]), ap(a[1])).then_inc(T.sem[a[2]], 16)
            return a[2], 16
        if kind == "store":
            Q[e].dma_start(hbm(a[1], a[2], a[0]), ap(a[0])).then_inc(T.sem.out, 16)
            return "out", 16
        x = [ap(v) for v in a]
        if kind == "cp":
            ins = g.vector.tensor_copy(*x)
        elif kind == "tt":
            ins = g.vector.tensor_tensor(*x)
        elif kind == "ts":
            ins = g.vector.tensor_scalar(*(x if x[5] is not None else x[:5]))
        elif kind == "scan":
            ins = g.vector.tensor_tensor_scan(*x)
        elif kind == "mset":
            ins = g.vector.memset(*x)
        elif kind == "act":
            ins = g.scalar.activation(x[0], x[1], x[2], bias=x[3], scale=x[4])
        elif kind == "mm":
            ins = g.tensor.matmul(*x)
        elif SCRATCH[a[0][0]][2] == "int32":
            ins = g.iota(*x)
        else:
            ins = g.iota(*x, allow_small_or_imprecise_dtypes=True)
        ins.then_inc(T.sem["s" + e], 1)
        return "s" + e, 1

    calls, dep, seq = planned()
    cnt, mark = {}, {}
    seen = {e: {} for e in Q}
    for i in seq:
        e, kind, args = calls[i][:3]
        if e != "r":
            need = {}
            for j, wait in dep[i].items():
                if wait:
                    s, c = mark[j]
                    need[s] = max(need.get(s, 0), c)
            for s in sorted(need):
                if seen[e].get(s, 0) < need[s]:
                    Q[e].wait_ge(T.sem[s], need[s])
                    seen[e][s] = need[s]
        s, inc = issue(e, kind, args)
        cnt[s] = cnt.get(s, 0) + inc
        mark[i] = (s, cnt[s])
    for s in sorted(cnt):
        g.wait_ge(T.sem[s], cnt[s])
